import numpy as np, ml_dtypes
CORES = [3,11,19,27,35,43,51,59]
N = 8
import mx_ref
BF = ml_dtypes.bfloat16
def entries(a):
    return np.ascontiguousarray(a.T).reshape(-1)
def table(e):
    return np.ascontiguousarray(np.reshape(e, (-1, 16)).T).astype(np.int32)
def cols(t, e):
    v = np.concatenate([t.reshape(128, -1, 4), np.zeros((128, 1, 4), BF)], axis=1)
    return np.ascontiguousarray(v[:, e]).reshape(128, -1)
def f(rng, *shape):
    return mx_ref.flush((rng.standard_normal(shape, dtype=np.float32) * np.exp2(rng.integers(-2, 3, shape[:-1] + (1,)))).astype(BF))
def wide(rng, *shape, cols=0):
    v = rng.standard_normal(shape, dtype=np.float32) * np.exp2(rng.integers(-12, 13, shape)).astype(np.float32)
    if cols: v *= np.repeat(np.exp2(rng.integers(-cols, cols + 1, shape[:-2] + (1, shape[-1] // 4))) * (rng.random(shape[:-2] + (1, shape[-1] // 4)) > 0.0625), 4, axis=-1).astype(np.float32)
    return mx_ref.flush(v.astype(BF))
TA, TB, CI, CJ, JW = 256, 256, 24, 64, 384
SIDE = [r // 4 for r in range(N)]
GCOL = [SIDE[:r].count(SIDE[r]) for r in range(N)]
def fill(rng, total, cap, wd, first, back):
    n = np.zeros(N, int)
    for q in first: n[q] = min(cap, total - n.sum())
    while n.sum() < total:
        q = rng.integers(0, N)
        if n[q] < cap: n[q] += 1
    s, used = np.full((N, cap), -1), []
    for q in range(N):
        k, v = rng.permutation(cap)[:n[q]], rng.integers(0, wd, n[q])
        if back: k, v = np.sort(k), np.sort(v)[::-1]
        s[q, k] = v; used += list(q * cap + k)
    return s, (np.sort(used)[::-1] if back else rng.permutation(used))
def lists(rng, full=False, own=False, back=False, alike=False):
    A, B = [], []
    for i in range(2):
        A.append(fill(rng, 128, CI, TA, rng.permutation(N) if full else [r for r in range(N) if own and SIDE[r] == i], back))
    for k in range(4):
        B.append(fill(rng, JW, CJ, TB, rng.permutation(N) if full else [r for r in range(N) if own and GCOL[r] == k], back))
    if alike: B = [B[0]] * 4
    return {"sa": np.stack([table(np.concatenate([A[i][0][q] for i in range(2)])) for q in range(N)]),
            "sb": np.stack([table(np.concatenate([B[k][0][q] for k in range(4)])) for q in range(N)]),
            "pi": np.stack([table(A[SIDE[r]][1]) for r in range(N)]), "pj": np.stack([table(B[GCOL[r]][1]) for r in range(N)])}
def setup_inputs(rng):
    return {"a": f(rng, N, 128, 4 * TA), "b": f(rng, N, 128, 4 * TB), **lists(rng)}
def setup_inputs_alike(rng):
    return {**setup_inputs(rng), **lists(rng, alike=True)}
def setup_inputs_full(rng):
    return {**setup_inputs(rng), **lists(rng, full=True)}
def setup_inputs_own(rng):
    return {**setup_inputs(rng), **lists(rng, own=True)}
def setup_inputs_reversed(rng):
    return {**setup_inputs(rng), **lists(rng, back=True)}
def setup_inputs_spread(rng):
    d = setup_inputs(rng); d["a"], d["b"] = wide(rng, N, 128, 4 * TA, cols=6), wide(rng, N, 128, 4 * TB, cols=6); return d
def check_inputs(d):
    bad = []
    for s, p, wd, cap, total, place in (("sa", "pi", TA, CI, 128, SIDE), ("sb", "pj", TB, CJ, JW, GCOL)):
        e = np.stack([entries(d[s][q]) for q in range(N)])
        if e.min() < -1 or e.max() >= wd: bad.append(s)
        for r in range(N):
            v = e[:, cap * place[r]:cap * place[r] + cap].reshape(-1)
            if (v >= 0).sum() != total: bad.append(s + " count")
            t = entries(d[p][r])
            if t.min() < 0 or t.max() >= N * cap: bad.append(p); continue
            if len(set(t.tolist())) != total or (v[t] < 0).any(): bad.append(p + " slots")
            if (d[p][r] != d[p][place.index(place[r])]).any(): bad.append(p + " not the same")
    return bad
def reference(a, b, sa, sb, pi, pj):
    y = np.zeros((N, 128, JW), np.float32)
    for r in range(N):
        i, k = SIDE[r], GCOL[r]
        A = np.concatenate([cols(a[q], entries(sa[q])[CI * i:CI * i + CI]) for q in range(N)], axis=1)
        B = np.concatenate([cols(b[q], entries(sb[q])[CJ * k:CJ * k + CJ]) for q in range(N)], axis=1)
        y[r] = mx_ref.matmul(mx_ref.quantize(cols(A, entries(pi[r]))), mx_ref.quantize(cols(B, entries(pj[r]))))
    return {"y": y}

@@ -1,0 +1,404 @@
+from concourse.bass import DstId, RemoteDMATransfer, IndirectOffsetOnAxis
+from concourse.mybir import dt, AluOpType, AxisListType, ActivationFunctionType
+
+CORES = [3, 11, 19, 27, 35, 43, 51, 59]
+N = 8
+TA, TB, CI, CJ, JW, M = 256, 256, 24, 64, 384, 128
+SIDE = [r // 4 for r in range(N)]
+GCOL = [r % 4 for r in range(N)]
+PAIR = 2 * CJ
+SA, SB = N * CI, N * CJ
+KB, KA = 16, 3
+LAW = 304
+ZA = 128 - 2 * CI
+CHUNKS = ((0, 3 * CJ), (3 * CJ, 5 * CJ), (5 * CJ, 8 * CJ))
+
+SCRATCH = {
+    "wa": ("sbuf", [128, 4 * TA], "bfloat16"),
+    "wb": ("sbuf", [128, 4 * TB], "bfloat16"),
+    "lsb": ("sbuf", [128, KB], "int32"),
+    "lsa": ("sbuf", [128, KA], "int32"),
+    "offb": ("sbuf", [128, 4 * KB], "uint16"),
+    "offa": ("sbuf", [128, 16], "uint16"),
+    "tf": ("sbuf", [128, 4 * PAIR], "bfloat16"),
+    "tn": ("sbuf", [128, 4 * PAIR], "bfloat16"),
+    "ta": ("sbuf", [128, 4 * 128], "bfloat16"),
+    "qc": ("sbuf", [128, PAIR], "float8_e4m3fn_x4"),
+    "qs": ("sbuf", [128, PAIR], "uint8"),
+    "hfc": ("sbuf", [128, CJ], "float8_e4m3fn_x4"),
+    "hfs": ("sbuf", [128, CJ], "uint8"),
+    "hnc": ("sbuf", [128, CJ], "float8_e4m3fn_x4"),
+    "hns": ("sbuf", [128, CJ], "uint8"),
+    "hac": ("sbuf", [128, 2 * CI], "float8_e4m3fn_x4"),
+    "has": ("sbuf", [128, 2 * CI], "uint8"),
+    "lac": ("sbuf", [128, LAW], "float8_e4m3fn_x4"),
+    "las": ("sbuf", [128, LAW], "uint8"),
+    "lbc": ("sbuf", [128, SB + CJ], "float8_e4m3fn_x4"),
+    "lbs": ("sbuf", [128, SB + CJ], "uint8"),
+    "pil": ("sbuf", [128, 8], "int32"),
+    "pit": ("sbuf", [128, 8], "int32"),
+    "pim": ("sbuf", [128, 8 * N], "int32"),
+    "pio": ("sbuf", [128, 8], "uint16"),
+    "pjl": ("sbuf", [128, 24], "int32"),
+    "pjt": ("sbuf", [128, 24], "int32"),
+    "pju": ("sbuf", [128, 24], "int32"),
+    "pjo": ("sbuf", [128, 24], "uint16"),
+    "part": ("sbuf", [128, 1], "int32"),
+    "part16": ("sbuf", [128, 1], "int32"),
+    "partf": ("sbuf", [128, 1], "float32"),
+    "count": ("sbuf", [128, 128], "float32"),
+    "eye": ("sbuf", [128, 128], "float32"),
+    "inv": ("sbuf", [128, LAW], "float32"),
+    "dg1": ("sbuf", [128, 128], "float32"),
+    "dg2": ("sbuf", [128, 128], "float32"),
+    "ix1f": ("sbuf", [128, 1], "float32"),
+    "ix2f": ("sbuf", [128, 1], "float32"),
+    "ix1": ("sbuf", [128, 1], "int32"),
+    "ix2": ("sbuf", [128, 1], "int32"),
+    "s1": ("sbuf", [128, SB], "float32"),
+    "s2": ("sbuf", [128, SB], "float32"),
+    "y1": ("sbuf", [128, JW], "float32"),
+    "y2": ("sbuf", [128, JW], "float32"),
+    "ps": ("psum", [128, 6 * 512], "float32"),
+}
+SEMAPHORES = ["listb", "lista", "ldb", "lda", "ldpi", "ldpj", "iota", "cnt", "filled", "zeros", "p16", "pf",
+              "off2", "off3", "offv", "offa", "fars", "farv", "nears", "nearv", "as", "av", "qf", "qn", "qa", "vc", "ixd",
+              "hfc", "hfs", "hnc", "hns", "hac", "has", "arre", "arrl", "arr0", "arr1", "arr2", "arr3", "sent",
+              "m0", "m1", "m2", "m3", "m4", "m5", "c1v", "c1s", "c2v", "c2s", "yd1", "yd2", "ystored"]
+
+
+def bland(d, q):
+    if GCOL[d] % 2 == 0:
+        return 0, (q - d - 1) % N
+    return CJ, (q - d) % N
+
+
+def near_at(r):
+    view, pos = bland(r, r)
+    return view + CJ * pos - CJ * (GCOL[r] % 2)
+
+
+def bsrc(q, d):
+    if GCOL[d] // 2 == GCOL[q] // 2:
+        return "lbc", "lbs", near_at(q) + CJ * (GCOL[d] % 2)
+    return "qc", "qs", CJ * (GCOL[d] % 2)
+
+
+def a_run(r):
+    return (176, 176) if SIDE[r] == 0 else (0, ZA)
+
+
+def away(d, q):
+    return (q // 2 - d // 2) % 4
+
+
+def groups(topo, q):
+    chip = [topo.chip(c) for c in CORES]
+    mate = [d for d in range(N) if topo.mates(chip[q], chip[d])][0]
+    same = [d for d in range(N) if d != q and topo.same_plane(chip[q], chip[d])]
+    cross = [d for d in range(N) if d not in same + [q, mate]]
+    near = lambda ds: [d for d in ds if GCOL[d] // 2 == GCOL[q] // 2]
+    far = lambda ds: [d for d in ds if GCOL[d] // 2 != GCOL[q] // 2]
+    return mate, near(same), far(same), near(cross), far(cross)
+
+
+def aland(topo, d):
+    mate, _, _, xn, _ = groups(topo, d)
+    late = [q for q in range(N) if q not in [d, mate] + xn]
+    order = late + xn + [mate, d] if SIDE[d] == 0 else [d, mate] + xn + late
+    first = 8 if SIDE[d] == 0 else ZA + CI
+    land = {q: first + CI * i for i, q in enumerate(order)}
+    if SIDE[d] == 0:
+        return land, (land[xn[0]], 3 * CI), (first, 5 * CI), 0
+    return land, (land[xn[0]] + CI - 128, 128), (first + SA - 128, 128), 128 - 5 * CI
+
+
+def plan(topo, q):
+    me = CORES[q]
+    mate, sn, sf, xn, xf = groups(topo, q)
+    others = [c for c in topo.cores_of(me) if c != me]
+    here = lambda cs: sorted(cs, key=lambda c: topo.die(c) != topo.die(me))
+    x1, x2, x3 = here([c for c in others if topo.may_write(c, CORES[mate])])[:3]
+    p = here([c for c in others if not topo.may_write(c, CORES[mate])])
+    s2, s1, s3 = p[0], p[2], p[1]
+    run = a_run(q)[1]
+    hops = {"hfc": [(x2, bsrc(q, xf[0])[2]), (s2, bsrc(q, sf[0])[2])], "hfs": [(x3, bsrc(q, xf[0])[2]), (s3, bsrc(q, sf[0])[2])],
+            "hnc": [(x1, bsrc(q, xn[0])[2]), (s1, bsrc(q, sn[0])[2])], "hns": [(x3, bsrc(q, xn[0])[2]), (s3, bsrc(q, sn[0])[2])],
+            "hac": [(x1, run), (s1, run)], "has": [(x2, run), (s2, run)]}
+    b = bsrc(q, mate)
+    sends = {me: [(None, "bc", [mate], b[0], b[2]), (None, "bs", [mate], b[1], b[2]),
+                  (None, "ac", [mate] + xn, "lac", run), (None, "as", [mate] + xn, "las", run)],
+             x1: [("hnc", "bc", xn, "hnc", 0), ("hac", "ac", xf, "hac", 0)],
+             s1: [("hnc", "bc", sn, "hnc", 0), ("hac", "ac", sf, "hac", 0), (None, "ac", sn, "hac", 0)],
+             x2: [("hfc", "bc", xf, "hfc", 0), ("has", "as", xf, "has", 0)],
+             s2: [("hfc", "bc", sf, "hfc", 0), ("has", "as", sf, "has", 0), (None, "as", sn, "has", 0)],
+             x3: [("hfs", "bs", xf, "hfs", 0), ("hns", "bs", xn, "hns", 0)],
+             s3: [("hfs", "bs", sf, "hfs", 0), ("hns", "bs", sn, "hns", 0)]}
+    return sends, hops
+
+
+def masks(topo, src, dsts):
+    e = topo.engines(src, dsts[0])
+    return [sum(1 << x for x in e[i::len(dsts)]) for i in range(len(dsts))]
+
+
+def engines_in(m):
+    return bin(m).count("1")
+
+
+def arrival_sem(topo, d, q, kind):
+    mate, _, _, xn, _ = groups(topo, d)
+    return "arr%d" % away(d, q) if kind[0] == "b" else "arre" if q in [mate] + xn else "arrl"
+
+
+def view(T, name, c, w):
+    return T[name][:, c:c + w].bitcast(dt.uint8) if name[-1] == "c" else T[name][:, c:c + w]
+
+
+def fused(g, T, topo, core, parts):
+    ms = masks(topo, core, [x[0] for x in parts])
+    tr = []
+    for (c, sem, w, s, sc, d, dc), m in zip(parts, ms):
+        rid, pid, _ = topo.addr(c)
+        tr.append(RemoteDMATransfer(dst_ids=[DstId(rid=rid, pnc=pid)], dma_engine_mask=m, remote_sem=T.sem[sem],
+                                    srcs=[view(T, s, sc, w)], dsts=[view(T, d, dc, w)], alu_op=0))
+    g.remote_dma_fused(tr, local_sem=T.sem.sent)
+    return sum(engines_in(m) for m in ms)
+
+
+def send(g, T, topo, core, q, call):
+    _, kind, dsts, src, c0 = call
+    parts = []
+    for d in dsts:
+        if kind[0] == "b":
+            v0, pos = bland(d, q)
+            w, c, e = CJ, c0, v0 + CJ * pos
+        else:
+            w, c, e = CI, c0 + CI * SIDE[d], aland(topo, d)[0][q]
+        parts.append((CORES[d], arrival_sem(topo, d, q, kind), w, src, c, "l" + kind, e))
+    return fused(g, T, topo, core, parts)
+
+
+def hop(g, T, topo, core, buf, src, to):
+    w = 2 * CI if buf[1] == "a" else CJ
+    return fused(g, T, topo, core, [(c, buf, w, src, col, buf, 0) for c, col in to])
+
+
+def arrivals(topo, r):
+    n = {}
+    for q in range(N):
+        for c, calls in plan(topo, q)[0].items():
+            for _, kind, dsts, _, _ in calls:
+                for d, m in zip(dsts, masks(topo, c, [CORES[x] for x in dsts])):
+                    if d == r:
+                        s = arrival_sem(topo, r, q, kind)
+                        n[s] = n.get(s, 0) + engines_in(m)
+    return n
+
+
+def helper_program(g, core, T, topo, q):
+    sends, hops = plan(topo, q)
+    used = 0
+    for call in sends.get(core, []):
+        if call[0]:
+            ms = masks(topo, CORES[q], [c for c, _ in hops[call[0]]])
+            g.wait_ge(T.sem[call[0]], [engines_in(m) for (c, _), m in zip(hops[call[0]], ms) if c == core][0])
+        used += send(g, T, topo, core, q, call)
+    if used:
+        g.wait_ge(T.sem.sent, used)
+
+
+def rank_program(g, core, T, topo):
+    rank = T.rank_of(core)
+    if rank is None:
+        q = [r for r in range(N) if topo.chip(CORES[r]) == topo.chip(core)]
+        if q:
+            helper_program(g, core, T, topo, q[0])
+        return
+    v, sc, sy, te, sem = g.vector, g.scalar, g.sync, g.tensor, T.sem
+    COPY, A = ActivationFunctionType.Copy, AluOpType
+    sends, hops = plan(topo, rank)
+    land, view1, view2, both = aland(topo, rank)
+    kn = 8 * (GCOL[rank] // 2)
+    kf = 8 - kn
+
+    sy.dma_start(T.wb[:], T.b[:]).then_inc(sem.ldb, 16)
+    for k in range(8):
+        (sy if k < 4 else sc).dma_start(T.lsb[16 * k:16 * k + 16, :], T.sb[:]).then_inc(sem.listb, 16)
+    sy.dma_start(T.wa[:], T.a[:]).then_inc(sem.lda, 16)
+    for k in range(8):
+        (sy if k < 4 else sc).dma_start(T.lsa[16 * k:16 * k + 16, :], T.sa[:]).then_inc(sem.lista, 16)
+    for k in range(8):
+        sy.dma_start(T.pil[16 * k:16 * k + 16, :], T.pi[:]).then_inc(sem.ldpi, 16)
+
+    g.iota(T.part[:], [[1, 1]], 0, 1).then_inc(sem.iota, 1)
+    g.iota(T.count[:], [[1, 128]], 0, 0, allow_small_or_imprecise_dtypes=True).then_inc(sem.cnt, 1)
+    g.wait_ge(sem.p16, 1)
+    g.indirect_dma_start(out=T.pjl[:, 0:24], out_offset=None, in_=T.pj[:],
+                         in_offset=IndirectOffsetOnAxis(ap=T.part16[:, 0:1], axis=0),
+                         bounds_check=15).then_inc(sem.ldpj, 16)
+    used = 0
+    for ready, codes, scales, src in (("qf", "hfc", "hfs", "q"), ("qn", "hnc", "hns", "lb"), ("qa", "hac", "has", "la")):
+        g.wait_ge(sem[ready], 1)
+        used += hop(g, T, topo, core, codes, src + "c", hops[codes])
+        used += hop(g, T, topo, core, scales, src + "s", hops[scales])
+    for call in sends[core]:
+        used += send(g, T, topo, core, rank, call)
+
+    run, ablk = a_run(rank)
+    za = 2 * CI if ablk == run else 0
+    v.memset(T.ta[:, 4 * za:4 * (za + ZA)], 0.0).then_inc(sem.zeros, 1)
+    v.wait_ge(sem.iota, 1)
+    v.tensor_scalar(T.part16[:], T.part[:], 15, None, A.bitwise_and).then_inc(sem.p16, 1)
+    v.tensor_copy(T.partf[:], T.part[:]).then_inc(sem.pf, 1)
+    v.memset(T.inv[:], 999.0).then_inc(sem.filled, 1)
+
+    def offsets(what, t, s):
+        out, lst, k, step = (T.offb, T.lsb, KB, KB) if what == "b" else (T.offa, T.lsa, KA, 4)
+        v.tensor_scalar(out[:, step * t:step * t + k], lst[:], 4, t, A.mult, A.add).then_inc(sem[s], 1)
+
+    def blocks(t, what):
+        if what == "a":
+            c = 4 * (ablk - run)
+            return T.ta[:, c + t:c + 8 * CI:4], T.wa[:].indirect(T.offa[:, 4 * t:4 * t + KA])
+        k = KB * t + (kn if what == "near" else kf)
+        return (T.tn if what == "near" else T.tf)[:, t:4 * PAIR:4], T.wb[:].indirect(T.offb[:, k:k + 8])
+
+    def gather_v(t, what, s):
+        o, i = blocks(t, what)
+        v.tensor_copy(o, i).then_inc(sem[s], 1)
+
+    def gather_s(t, what, s):
+        o, i = blocks(t, what)
+        sc.activation(o, i, COPY).then_inc(sem[s], 1)
+
+    v.wait_ge(sem.listb, 128)
+    offsets("b", 2, "off2")
+    offsets("b", 3, "off3")
+    offsets("b", 0, "offv")
+    offsets("b", 1, "offv")
+    sc.wait_ge(sem.ldb, 16)
+    sc.wait_ge(sem.off2, 1)
+    gather_s(2, "far", "fars")
+    sc.wait_ge(sem.off3, 1)
+    gather_s(3, "far", "fars")
+    sc.wait_ge(sem.offv, 2)
+    for t in (1, 2, 3):
+        gather_s(t, "near", "nears")
+    v.wait_ge(sem.offv, 2)
+    v.wait_ge(sem.ldb, 16)
+    gather_v(0, "far", "farv")
+    gather_v(1, "far", "farv")
+    v.wait_ge(sem.farv, 2)
+    v.wait_ge(sem.fars, 2)
+    v.quantize_mx(T.qc[:], T.qs[:], T.tf[:]).then_inc(sem.qf, 1)
+    gather_v(0, "near", "nearv")
+    v.wait_ge(sem.lista, 128)
+    for t in (2, 3, 0, 1):
+        offsets("a", t, "offa")
+    v.wait_ge(sem.nearv, 1)
+    v.wait_ge(sem.nears, 3)
+    e = near_at(rank)
+    v.quantize_mx(T.lbc[:, e:e + PAIR], T.lbs[:, e:e + PAIR], T.tn[:]).then_inc(sem.qn, 1)
+    sc.wait_ge(sem.offa, 4)
+    sc.wait_ge(sem.lda, 16)
+    v.wait_ge(sem.offa, 4)
+    v.wait_ge(sem.lda, 16)
+    gather_s(2, "a", "as")
+    gather_s(3, "a", "as")
+    gather_v(0, "a", "av")
+    gather_v(1, "a", "av")
+    v.wait_ge(sem.zeros, 1)
+    v.wait_ge(sem.av, 2)
+    v.wait_ge(sem["as"], 2)
+    v.quantize_mx(T.lac[:, run:run + 128], T.las[:, run:run + 128], T.ta[:]).then_inc(sem.qa, 1)
+
+    n = [0]
+
+    def done(ins):
+        ins.then_inc(sem.vc, 1)
+        n[0] += 1
+
+    def settle():
+        v.wait_ge(sem.vc, n[0])
+    shift = [land[q] - CI * q for q in range(N)]
+    jumps = [q for q in range(1, N) if shift[q] != shift[q - 1]]
+    v.wait_ge(sem.ldpj, 16)
+    done(v.tensor_scalar(T.pjt[:], T.pjl[:], CJ * bland(rank, 0)[1], None, A.add))
+    v.wait_ge(sem.ldpi, 128)
+    done(v.tensor_scalar(T.pit[:], T.pil[:], shift[0], None, A.add))
+    for q in jumps:
+        done(v.tensor_scalar(T.pim[:, 8 * q:8 * q + 8], T.pil[:], CI * q, shift[q] - shift[q - 1], A.is_ge, A.mult))
+    settle()
+    done(v.tensor_scalar(T.pju[:], T.pjt[:], SB - 1, None, A.bitwise_and))
+    for q in jumps:
+        done(v.tensor_tensor(T.pit[:], T.pit[:], T.pim[:, 8 * q:8 * q + 8], A.add))
+        settle()
+    done(v.tensor_copy(T.pio[:], T.pit[:]))
+    done(v.tensor_copy(T.pjo[:], T.pju[:]))
+    settle()
+    sc.wait_ge(sem.vc, n[0])
+    v.wait_ge(sem.filled, 1)
+    v.wait_ge(sem.cnt, 1)
+    done(v.tensor_copy(T.inv[:].indirect(T.pio[:, 0:8]), T.count[:]))
+    v.wait_ge(sem.pf, 1)
+    done(v.tensor_scalar(T.eye[:], T.count[:], T.partf[:, 0:1], None, A.is_equal))
+    settle()
+    for dg, (c, _) in (("dg1", view1), ("dg2", view2)):
+        done(v.tensor_tensor(T[dg][:], T.inv[:, c:c + 128], T.eye[:], A.mult))
+    settle()
+    done(v.tensor_reduce(T.ix1f[:], T.dg1[:], AxisListType.X, A.add))
+    done(v.tensor_reduce(T.ix2f[:], T.dg2[:], AxisListType.X, A.add))
+    settle()
+    if both:
+        done(v.memset(T.ix2f[0:both, :], 999.0))
+        settle()
+    v.tensor_copy(T.ix1[:], T.ix1f[:]).then_inc(sem.ixd, 1)
+    v.tensor_copy(T.ix2[:], T.ix2f[:]).then_inc(sem.ixd, 1)
+
+    counts = arrivals(topo, rank)
+    v0 = bland(rank, rank)[0]
+    lead = GCOL[rank] % 2 == 0
+    order = (0, 2, 1)
+    need = {0: ["arr1"] + (["arr0"] if lead else []), 2: ["arr3"] + ([] if lead else ["arr0"]), 1: ["arr2"]}
+    te.wait_ge(sem.qn, 1)
+    te.wait_ge(sem.qa, 1)
+    te.wait_ge(sem.arre, counts["arre"])
+    for i in range(6):
+        if i < 3:
+            for s in need[order[i]]:
+                te.wait_ge(sem[s], counts[s])
+        if i == 3:
+            te.wait_ge(sem.arrl, counts["arrl"])
+        a0 = (view1 if i < 3 else view2)[0]
+        b0, b1 = CHUNKS[order[i % 3]]
+        te.matmul_mx(T.ps[:, 512 * i:512 * i + b1 - b0], T.lac[:, a0:a0 + 128], T.las[:, a0:a0 + 128],
+                     T.lbc[:, v0 + b0:v0 + b1], T.lbs[:, v0 + b0:v0 + b1], True, True).then_inc(sem["m%d" % i], 1)
+    for i in (1, 2):
+        s, y, hy = T["s%d" % i], T["y%d" % i], JW // 2
+        cv, cs, yd = sem["c%dv" % i], sem["c%ds" % i], sem["yd%d" % i]
+        for k in range(3):
+            m = 3 * (i - 1) + k
+            b0, b1 = CHUNKS[order[k]]
+            src, dst = T.ps[:, 512 * m:512 * m + b1 - b0], s[:, b0:b1]
+            if k == 0:
+                sc.wait_ge(sem["m%d" % m], 1)
+                sc.activation(dst, src, COPY).then_inc(cs, 1)
+            else:
+                v.wait_ge(sem["m%d" % m], 1)
+                v.tensor_copy(dst, src).then_inc(cv, 1)
+        v.wait_ge(cv, 2)
+        v.wait_ge(cs, 1)
+        v.tensor_copy(y[:, 0:hy], s[:].indirect(T.pjo[:, 0:12])).then_inc(yd, 1)
+        sc.wait_ge(cv, 2)
+        sc.wait_ge(cs, 1)
+        sc.activation(y[:, hy:JW], s[:].indirect(T.pjo[:, 12:24]), COPY).then_inc(yd, 1)
+
+    g.wait_ge(sem.ixd, 2)
+    for i, rows in ((1, view1[1]), (2, view2[1])):
+        g.wait_ge(sem["yd%d" % i], 2)
+        g.indirect_dma_start(out=T.y[:], out_offset=IndirectOffsetOnAxis(ap=T["ix%d" % i][0:rows, 0:1], axis=0),
+                             in_=T["y%d" % i][0:rows, 0:JW], in_offset=None, bounds_check=M - 1,
+                             oob_is_err=False).then_inc(sem.ystored, 16)
+    g.wait_ge(sem.sent, used)
+    g.wait_ge(sem.ystored, 32)

@@ -7,48 +7,48 @@ TA, TB, CI, CJ, JW, M = 256, 256, 24, 64, 384, 128
 SIDE = [r // 4 for r in range(N)]
 GCOL = [r % 4 for r in range(N)]
 PAIR = 2 * CJ
-SA, SB = N * CI, N * CJ
-KB, KA = 16, 3
-LAW = 304
-ZA = 128 - 2 * CI
-CHUNKS = ((0, 3 * CJ), (3 * CJ, 5 * CJ), (5 * CJ, 8 * CJ))
+SB = N * CJ
+KB, KA, KL = 16, 3, 20
+BA = CJ + CI
+SPARE = 128 - 5 * CI
+
+FAR = 0
+SN = FAR + PAIR
+TILE1 = SN + CJ
+XN = TILE1 + 128 - CI
+OWN = XN + BA
+MIX = OWN + CJ
+MIXW = BA + 3 * CI
+FARB = MIX + MIXW + SPARE
+MATE = FARB + 2 * PAIR
+TILE2 = MATE + CJ
+ZERO = TILE2 + 5 * CI
+LW = ZERO + 128
 
 SCRATCH = {
     "wa": ("sbuf", [128, 4 * TA], "bfloat16"),
     "wb": ("sbuf", [128, 4 * TB], "bfloat16"),
-    "lsb": ("sbuf", [128, KB], "int32"),
-    "lsa": ("sbuf", [128, KA], "int32"),
-    "offb": ("sbuf", [128, 4 * KB], "uint16"),
-    "offa": ("sbuf", [128, 16], "uint16"),
+    "lists": ("sbuf", [128, KL], "int32"),
+    "off": ("sbuf", [128, 4 * KL], "uint16"),
     "tf": ("sbuf", [128, 4 * PAIR], "bfloat16"),
-    "tn": ("sbuf", [128, 4 * PAIR], "bfloat16"),
-    "ta": ("sbuf", [128, 4 * 128], "bfloat16"),
-    "qc": ("sbuf", [128, PAIR], "float8_e4m3fn_x4"),
-    "qs": ("sbuf", [128, PAIR], "uint8"),
+    "tn": ("sbuf", [128, 4 * (CJ + MIXW)], "bfloat16"),
+    "tz": ("sbuf", [128, 4 * 128], "bfloat16"),
     "hfc": ("sbuf", [128, CJ], "float8_e4m3fn_x4"),
     "hfs": ("sbuf", [128, CJ], "uint8"),
-    "hnc": ("sbuf", [128, CJ], "float8_e4m3fn_x4"),
-    "hns": ("sbuf", [128, CJ], "uint8"),
     "hac": ("sbuf", [128, 2 * CI], "float8_e4m3fn_x4"),
     "has": ("sbuf", [128, 2 * CI], "uint8"),
-    "lac": ("sbuf", [128, LAW], "float8_e4m3fn_x4"),
-    "las": ("sbuf", [128, LAW], "uint8"),
-    "lbc": ("sbuf", [128, SB + CJ], "float8_e4m3fn_x4"),
-    "lbs": ("sbuf", [128, SB + CJ], "uint8"),
-    "pil": ("sbuf", [128, 8], "int32"),
-    "pit": ("sbuf", [128, 8], "int32"),
-    "pim": ("sbuf", [128, 8 * N], "int32"),
-    "pio": ("sbuf", [128, 8], "uint16"),
+    "hmc": ("sbuf", [128, BA + SPARE], "float8_e4m3fn_x4"),
+    "lc": ("sbuf", [128, LW], "float8_e4m3fn_x4"),
+    "ls": ("sbuf", [128, LW], "uint8"),
     "pjl": ("sbuf", [128, 24], "int32"),
-    "pjt": ("sbuf", [128, 24], "int32"),
-    "pju": ("sbuf", [128, 24], "int32"),
+    "pirow": ("sbuf", [128, M], "int32"),
+    "piall": ("sbuf", [128, M], "int32"),
+    "step": ("sbuf", [128, 24], "float32"),
     "pjo": ("sbuf", [128, 24], "uint16"),
-    "part": ("sbuf", [128, 1], "int32"),
-    "part16": ("sbuf", [128, 1], "int32"),
     "partf": ("sbuf", [128, 1], "float32"),
     "count": ("sbuf", [128, 128], "float32"),
-    "eye": ("sbuf", [128, 128], "float32"),
-    "inv": ("sbuf", [128, LAW], "float32"),
+    "frac": ("sbuf", [128, 128], "float32"),
+    "both": ("sbuf", [128, 128], "float32"),
     "dg1": ("sbuf", [128, 128], "float32"),
     "dg2": ("sbuf", [128, 128], "float32"),
     "ix1f": ("sbuf", [128, 1], "float32"),
@@ -59,37 +59,13 @@ SCRATCH = {
     "s2": ("sbuf", [128, SB], "float32"),
     "y1": ("sbuf", [128, JW], "float32"),
     "y2": ("sbuf", [128, JW], "float32"),
-    "ps": ("psum", [128, 6 * 512], "float32"),
+    "ps": ("psum", [128, 8 * 512], "float32"),
 }
-SEMAPHORES = ["listb", "lista", "ldb", "lda", "ldpi", "ldpj", "iota", "cnt", "filled", "zeros", "p16", "pf",
-              "off2", "off3", "offv", "offa", "fars", "farv", "nears", "nearv", "as", "av", "qf", "qn", "qa", "vc", "ixd",
-              "hfc", "hfs", "hnc", "hns", "hac", "has", "arre", "arrl", "arr0", "arr1", "arr2", "arr3", "sent",
-              "m0", "m1", "m2", "m3", "m4", "m5", "c1v", "c1s", "c2v", "c2s", "yd1", "yd2", "ystored"]
-
-
-def bland(d, q):
-    if GCOL[d] % 2 == 0:
-        return 0, (q - d - 1) % N
-    return CJ, (q - d) % N
-
-
-def near_at(r):
-    view, pos = bland(r, r)
-    return view + CJ * pos - CJ * (GCOL[r] % 2)
-
-
-def bsrc(q, d):
-    if GCOL[d] // 2 == GCOL[q] // 2:
-        return "lbc", "lbs", near_at(q) + CJ * (GCOL[d] % 2)
-    return "qc", "qs", CJ * (GCOL[d] % 2)
-
-
-def a_run(r):
-    return (176, 176) if SIDE[r] == 0 else (0, ZA)
-
-
-def away(d, q):
-    return (q // 2 - d // 2) % 4
+SEMAPHORES = ["listb", "lista", "spread", "ldb", "lda", "ldpi", "ldpj", "cnt", "filled", "zeros", "cast",
+              "off0", "off1", "off2", "off3", "offas", "offav", "fars", "farv", "nears", "nearv", "as", "av", "owns", "ownv",
+              "qz", "qf", "qn", "qo", "vc", "ixd", "go", "moved", "hfc", "hfs", "hac", "has", "hmc",
+              "mate", "near", "far0", "far1", "late", "sent",
+              "m0", "m1", "m2", "m3", "m4", "m5", "m6", "m7", "m8", "c1v", "c1s", "c2v", "c2s", "yd1", "yd2", "ystored"]
 
 
 def groups(topo, q):
@@ -99,18 +75,21 @@ def groups(topo, q):
     cross = [d for d in range(N) if d not in same + [q, mate]]
     near = lambda ds: [d for d in ds if GCOL[d] // 2 == GCOL[q] // 2]
     far = lambda ds: [d for d in ds if GCOL[d] // 2 != GCOL[q] // 2]
-    return mate, near(same), far(same), near(cross), far(cross)
+    return mate, near(same)[0], far(same), near(cross)[0], far(cross)
 
 
-def aland(topo, d):
-    mate, _, _, xn, _ = groups(topo, d)
-    late = [q for q in range(N) if q not in [d, mate] + xn]
-    order = late + xn + [mate, d] if SIDE[d] == 0 else [d, mate] + xn + late
-    first = 8 if SIDE[d] == 0 else ZA + CI
-    land = {q: first + CI * i for i, q in enumerate(order)}
-    if SIDE[d] == 0:
-        return land, (land[xn[0]], 3 * CI), (first, 5 * CI), 0
-    return land, (land[xn[0]] + CI - 128, 128), (first + SA - 128, 128), 128 - 5 * CI
+def sides_at(q):
+    return BA + CI * SIDE[q]
+
+
+def places(topo, d):
+    mate, sn, sf, xn, xf = groups(topo, d)
+    far = sorted(sf + xf)
+    b = {sn: SN, xn: XN + CI, d: OWN, mate: MATE}
+    a = {sn: TILE1, d: TILE1 + CI, xn: XN, mate: TILE2}
+    b.update({q: FARB + CJ * i for i, q in enumerate(sf + xf)})
+    a.update({q: TILE2 + CI + CI * i for i, q in enumerate(far)})
+    return b, a
 
 
 def plan(topo, q):
@@ -120,198 +99,196 @@ def plan(topo, q):
     here = lambda cs: sorted(cs, key=lambda c: topo.die(c) != topo.die(me))
     x1, x2, x3 = here([c for c in others if topo.may_write(c, CORES[mate])])[:3]
     p = here([c for c in others if not topo.may_write(c, CORES[mate])])
-    s2, s1, s3 = p[0], p[2], p[1]
-    run = a_run(q)[1]
-    hops = {"hfc": [(x2, bsrc(q, xf[0])[2]), (s2, bsrc(q, sf[0])[2])], "hfs": [(x3, bsrc(q, xf[0])[2]), (s3, bsrc(q, sf[0])[2])],
-            "hnc": [(x1, bsrc(q, xn[0])[2]), (s1, bsrc(q, sn[0])[2])], "hns": [(x3, bsrc(q, xn[0])[2]), (s3, bsrc(q, sn[0])[2])],
-            "hac": [(x1, run), (s1, run)], "has": [(x2, run), (s2, run)]}
-    b = bsrc(q, mate)
-    sends = {me: [(None, "bc", [mate], b[0], b[2]), (None, "bs", [mate], b[1], b[2]),
-                  (None, "ac", [mate] + xn, "lac", run), (None, "as", [mate] + xn, "las", run)],
-             x1: [("hnc", "bc", xn, "hnc", 0), ("hac", "ac", xf, "hac", 0)],
-             s1: [("hnc", "bc", sn, "hnc", 0), ("hac", "ac", sf, "hac", 0), (None, "ac", sn, "hac", 0)],
-             x2: [("hfc", "bc", xf, "hfc", 0), ("has", "as", xf, "has", 0)],
-             s2: [("hfc", "bc", sf, "hfc", 0), ("has", "as", sf, "has", 0), (None, "as", sn, "has", 0)],
-             x3: [("hfs", "bs", xf, "hfs", 0), ("hns", "bs", xn, "hns", 0)],
-             s3: [("hfs", "bs", sf, "hfs", 0), ("hns", "bs", sn, "hns", 0)]}
-    return sends, hops
+    s2, s1 = p[0], p[-1]
+    fcol = lambda ds: FAR + CJ * (GCOL[ds[0]] % 2)
+    both = MIX + sides_at(q)
+
+    def far(k, ds):
+        return [(CORES[d], "far%d" % (ds == xf), CJ, "hf" + k, 0, "l" + k, places(topo, d)[0][q]) for d in ds]
+
+    def late(k, ds):
+        return [(CORES[d], "late", CI, "ha" + k, CI * SIDE[d], "l" + k, places(topo, d)[1][q]) for d in ds]
+
+    def near(k):
+        return [(CORES[sn], "near", BA, "l" + k, OWN, "l" + k, SN), (CORES[xn], "near", BA, "l" + k, MIX, "l" + k, XN)]
+
+    def last(k):
+        return [(CORES[mate], "mate", BA, "l" + k, MIX + CI, "l" + k, MATE)]
+
+    def hop(buf, w, to):
+        return [(c, buf, w, "l" + buf[-1], col, buf, 0) for c, col in to]
+    return {me: [("qf", hop("hfc", CJ, [(x2, fcol(xf)), (s2, fcol(sf))])),
+                 (None, hop("hfs", CJ, [(x1, fcol(xf)), (s1, fcol(sf))])),
+                 ("qn", []),
+                 ("beside", hop("hac", 2 * CI, [(x3, both), (s1, both)])),
+                 ("qo", near("c") + hop("hmc", BA, [(x1, MIX + CI)])),
+                 ("beside", hop("has", 2 * CI, [(x2, both), (s2, both)])),
+                 (None, near("s")), ("go", last("s"))],
+            x1: [("hfs", far("s", xf)), ("hmc", [(CORES[mate], "mate", BA, "hmc", 0, "lc", MATE)])],
+            x2: [("hfc", far("c", xf)), ("has", late("s", xf))],
+            x3: [("hac", late("c", xf))],
+            s2: [("hfc", far("c", sf)), ("has", late("s", sf))],
+            s1: [("hfs", far("s", sf)), ("hac", late("c", sf))]}
 
 
-def masks(topo, src, dsts):
-    e = topo.engines(src, dsts[0])
-    return [sum(1 << x for x in e[i::len(dsts)]) for i in range(len(dsts))]
+def masks(topo, src, parts, beside=False):
+    off = [i for i, x in enumerate(parts) if topo.chip(x[0]) != topo.chip(src)]
+    on = [i for i in range(len(parts)) if i not in off]
+    plane = [c for c in CORES if topo.same_plane(topo.chip(c), topo.chip(src))]
+    eoff = topo.engines(src, plane[0]) if off or beside in ("beside", "below") else []
+    eon = [e for e in topo.engines(src, parts[on[0]][0]) if (e in eoff) == (beside == "below")] if on else []
+    share = {i: e[k::len(xs)] for xs, e in ((off, eoff), (on, eon)) for k, i in enumerate(xs)}
+    return [sum(1 << e for e in share[i]) for i in range(len(parts))]
 
 
 def engines_in(m):
     return bin(m).count("1")
 
 
-def arrival_sem(topo, d, q, kind):
-    mate, _, _, xn, _ = groups(topo, d)
-    return "arr%d" % away(d, q) if kind[0] == "b" else "arre" if q in [mate] + xn else "arrl"
-
-
 def view(T, name, c, w):
     return T[name][:, c:c + w].bitcast(dt.uint8) if name[-1] == "c" else T[name][:, c:c + w]
 
 
-def fused(g, T, topo, core, parts):
-    ms = masks(topo, core, [x[0] for x in parts])
-    tr = []
-    for (c, sem, w, s, sc, d, dc), m in zip(parts, ms):
-        rid, pid, _ = topo.addr(c)
-        tr.append(RemoteDMATransfer(dst_ids=[DstId(rid=rid, pnc=pid)], dma_engine_mask=m, remote_sem=T.sem[sem],
-                                    srcs=[view(T, s, sc, w)], dsts=[view(T, d, dc, w)], alu_op=0))
-    g.remote_dma_fused(tr, local_sem=T.sem.sent)
-    return sum(engines_in(m) for m in ms)
-
-
-def send(g, T, topo, core, q, call):
-    _, kind, dsts, src, c0 = call
-    parts = []
-    for d in dsts:
-        if kind[0] == "b":
-            v0, pos = bland(d, q)
-            w, c, e = CJ, c0, v0 + CJ * pos
-        else:
-            w, c, e = CI, c0 + CI * SIDE[d], aland(topo, d)[0][q]
-        parts.append((CORES[d], arrival_sem(topo, d, q, kind), w, src, c, "l" + kind, e))
-    return fused(g, T, topo, core, parts)
-
-
-def hop(g, T, topo, core, buf, src, to):
-    w = 2 * CI if buf[1] == "a" else CJ
-    return fused(g, T, topo, core, [(c, buf, w, src, col, buf, 0) for c, col in to])
-
-
-def arrivals(topo, r):
+def arrivals(topo, core):
     n = {}
     for q in range(N):
-        for c, calls in plan(topo, q)[0].items():
-            for _, kind, dsts, _, _ in calls:
-                for d, m in zip(dsts, masks(topo, c, [CORES[x] for x in dsts])):
-                    if d == r:
-                        s = arrival_sem(topo, r, q, kind)
-                        n[s] = n.get(s, 0) + engines_in(m)
+        for c, calls in plan(topo, q).items():
+            for ready, parts in calls:
+                for x, m in zip(parts, masks(topo, c, parts, ready) if parts else []):
+                    if x[0] == core:
+                        n[x[1]] = n.get(x[1], 0) + engines_in(m)
     return n
 
 
-def helper_program(g, core, T, topo, q):
-    sends, hops = plan(topo, q)
-    used = 0
-    for call in sends.get(core, []):
-        if call[0]:
-            ms = masks(topo, CORES[q], [c for c, _ in hops[call[0]]])
-            g.wait_ge(T.sem[call[0]], [engines_in(m) for (c, _), m in zip(hops[call[0]], ms) if c == core][0])
-        used += send(g, T, topo, core, q, call)
-    if used:
-        g.wait_ge(T.sem.sent, used)
+def remote_calls(g, core, T, topo, q):
+    counts, used = arrivals(topo, core), 0
+    for ready, parts in plan(topo, q).get(core, []):
+        if ready == "go":
+            g.sem_inc(T.sem.go, 1)
+        elif ready and ready not in ("beside", "below"):
+            g.wait_ge(T.sem[ready], counts.get(ready, 1))
+        if not parts:
+            continue
+        tr = []
+        for (c, sem, w, s, sc, d, dc), m in zip(parts, masks(topo, core, parts, ready)):
+            rid, pid, _ = topo.addr(c)
+            tr.append(RemoteDMATransfer(dst_ids=[DstId(rid=rid, pnc=pid)], dma_engine_mask=m, remote_sem=T.sem[sem],
+                                        srcs=[view(T, s, sc, w)], dsts=[view(T, d, dc, w)], alu_op=0))
+            used += engines_in(m)
+        g.remote_dma_fused(tr, local_sem=T.sem.sent)
+    return used
 
 
 def rank_program(g, core, T, topo):
     rank = T.rank_of(core)
     if rank is None:
         q = [r for r in range(N) if topo.chip(CORES[r]) == topo.chip(core)]
-        if q:
-            helper_program(g, core, T, topo, q[0])
+        used = remote_calls(g, core, T, topo, q[0]) if q else 0
+        if used:
+            g.wait_ge(T.sem.sent, used)
         return
     v, sc, sy, te, sem = g.vector, g.scalar, g.sync, g.tensor, T.sem
     COPY, A = ActivationFunctionType.Copy, AluOpType
-    sends, hops = plan(topo, rank)
-    land, view1, view2, both = aland(topo, rank)
-    kn = 8 * (GCOL[rank] // 2)
-    kf = 8 - kn
+    mate, sn, sf, xn, xf = groups(topo, rank)
+    far = sorted(sf + xf)
+    bat, aat = places(topo, rank)
+    side, both = SIDE[rank], sides_at(rank)
+    mixw = both + 2 * CI
 
+    for k in range(2):
+        (sy, sc)[k].dma_start(T.lists[16 * k:16 * k + 16, 0:KB], T.sb[:]).then_inc(sem.listb, 16)
     sy.dma_start(T.wb[:], T.b[:]).then_inc(sem.ldb, 16)
     for k in range(8):
-        (sy if k < 4 else sc).dma_start(T.lsb[16 * k:16 * k + 16, :], T.sb[:]).then_inc(sem.listb, 16)
-    sy.dma_start(T.wa[:], T.a[:]).then_inc(sem.lda, 16)
+        (sy, sc)[k % 2].dma_start(T.lists[16 * k:16 * k + 16, KB:KB + KA], T.sa[:]).then_inc(sem.lista, 16)
+    sc.dma_start(T.wa[:], T.a[:]).then_inc(sem.lda, 16)
     for k in range(8):
-        (sy if k < 4 else sc).dma_start(T.lsa[16 * k:16 * k + 16, :], T.sa[:]).then_inc(sem.lista, 16)
-    for k in range(8):
-        sy.dma_start(T.pil[16 * k:16 * k + 16, :], T.pi[:]).then_inc(sem.ldpi, 16)
+        sy.dma_start(T.pjl[16 * k:16 * k + 16, :], T.pj[:]).then_inc(sem.ldpj, 16)
 
-    g.iota(T.part[:], [[1, 1]], 0, 1).then_inc(sem.iota, 1)
-    g.iota(T.count[:], [[1, 128]], 0, 0, allow_small_or_imprecise_dtypes=True).then_inc(sem.cnt, 1)
-    g.wait_ge(sem.p16, 1)
-    g.indirect_dma_start(out=T.pjl[:, 0:24], out_offset=None, in_=T.pj[:],
-                         in_offset=IndirectOffsetOnAxis(ap=T.part16[:, 0:1], axis=0),
-                         bounds_check=15).then_inc(sem.ldpj, 16)
-    used = 0
-    for ready, codes, scales, src in (("qf", "hfc", "hfs", "q"), ("qn", "hnc", "hns", "lb"), ("qa", "hac", "has", "la")):
-        g.wait_ge(sem[ready], 1)
-        used += hop(g, T, topo, core, codes, src + "c", hops[codes])
-        used += hop(g, T, topo, core, scales, src + "s", hops[scales])
-    for call in sends[core]:
-        used += send(g, T, topo, core, rank, call)
+    g.iota(T.partf[:], [[1, 1]], 0, 1, allow_small_or_imprecise_dtypes=True).then_inc(sem.cnt, 1)
+    g.iota(T.count[:], [[1, 16], [16, 8]], 0, 0, allow_small_or_imprecise_dtypes=True).then_inc(sem.cnt, 1)
+    g.dma_start(T.pirow[0:1, :], T.pi[:]).then_inc(sem.ldpi, 16)
+    used = remote_calls(g, core, T, topo, rank)
+    g.wait_ge(sem.ldpi, 16)
+    g.partition_broadcast(T.piall[:], T.pirow[0:1, :], 128).then_inc(sem.cast, 1)
 
-    run, ablk = a_run(rank)
-    za = 2 * CI if ablk == run else 0
-    v.memset(T.ta[:, 4 * za:4 * (za + ZA)], 0.0).then_inc(sem.zeros, 1)
-    v.wait_ge(sem.iota, 1)
-    v.tensor_scalar(T.part16[:], T.part[:], 15, None, A.bitwise_and).then_inc(sem.p16, 1)
-    v.tensor_copy(T.partf[:], T.part[:]).then_inc(sem.pf, 1)
-    v.memset(T.inv[:], 999.0).then_inc(sem.filled, 1)
+    sy.wait_ge(sem.qz, 1)
+    for name in ("lc", "ls"):
+        sy.dma_start(view(T, name, TILE1 + 2 * CI, 128 - 3 * CI), view(T, name, ZERO, 128 - 3 * CI)).then_inc(sem.moved, 16)
+    sy.wait_ge(sem.qn, 1)
+    sy.wait_ge(sem.go, 1)
+    for name in ("lc", "ls"):
+        sy.dma_start(view(T, name, TILE1 + CI, CI), view(T, name, MIX + BA, CI)).then_inc(sem.moved, 16)
 
-    def offsets(what, t, s):
-        out, lst, k, step = (T.offb, T.lsb, KB, KB) if what == "b" else (T.offa, T.lsa, KA, 4)
-        v.tensor_scalar(out[:, step * t:step * t + k], lst[:], 4, t, A.mult, A.add).then_inc(sem[s], 1)
+    v.memset(T.tz[:], 0.0).then_inc(sem.zeros, 1)
+    v.wait_ge(sem.zeros, 1)
+    v.quantize_mx(T.lc[:, ZERO:LW], T.ls[:, ZERO:LW], T.tz[:]).then_inc(sem.qz, 1)
+    v.wait_ge(sem.cnt, 2)
+    v.tensor_scalar(T.frac[:], T.count[:], 1.0 / 256, None, A.mult).then_inc(sem.filled, 1)
 
-    def blocks(t, what):
-        if what == "a":
-            c = 4 * (ablk - run)
-            return T.ta[:, c + t:c + 8 * CI:4], T.wa[:].indirect(T.offa[:, 4 * t:4 * t + KA])
-        k = KB * t + (kn if what == "near" else kf)
-        return (T.tn if what == "near" else T.tf)[:, t:4 * PAIR:4], T.wb[:].indirect(T.offb[:, k:k + 8])
+    pieces = {"far": (T.tf, 0, T.wb, 8 - 8 * (GCOL[rank] // 2), 8), "own": (T.tn, 0, T.wb, 4 * GCOL[rank], 4),
+              "near": (T.tn, BA, T.wb, 4 * GCOL[mate], 4), "a": (T.tn, CJ + both, T.wa, KB, KA)}
 
-    def gather_v(t, what, s):
-        o, i = blocks(t, what)
-        v.tensor_copy(o, i).then_inc(sem[s], 1)
+    def offsets(ts, k0, k1, s):
+        for t in ts:
+            v.tensor_scalar(T.off[:, KL * t + k0:KL * t + k1], T.lists[:, k0:k1], 4, t, A.mult, A.add).then_inc(sem[s], 1)
 
-    def gather_s(t, what, s):
-        o, i = blocks(t, what)
-        sc.activation(o, i, COPY).then_inc(sem[s], 1)
+    def move(who, o, i, s):
+        (v.tensor_copy(o, i) if who == "v" else sc.activation(o, i, COPY)).then_inc(sem[s + who], 1)
 
-    v.wait_ge(sem.listb, 128)
-    offsets("b", 2, "off2")
-    offsets("b", 3, "off3")
-    offsets("b", 0, "offv")
-    offsets("b", 1, "offv")
+    def gather(who, what, ts):
+        tile, c, win, k, n = pieces[what]
+        for t in ts:
+            move(who, tile[:, 4 * c + t:4 * (c + 16 * n):4], win[:].indirect(T.off[:, KL * t + k:KL * t + k + n]), what)
+
+    def block(c):
+        return T.tn[:, 4 * (CJ + c):4 * (CJ + c + CI)]
+
+    v.wait_ge(sem.listb, 32)
+    for p in (32, 64, 96):
+        v.tensor_copy(T.lists[p:p + 32, 0:KB], T.lists[0:32, 0:KB]).then_inc(sem.spread, 1)
+    v.wait_ge(sem.spread, 3)
+    for t in (2, 0, 3, 1):
+        offsets((t,), 0, KB, "off%d" % t)
     sc.wait_ge(sem.ldb, 16)
-    sc.wait_ge(sem.off2, 1)
-    gather_s(2, "far", "fars")
-    sc.wait_ge(sem.off3, 1)
-    gather_s(3, "far", "fars")
-    sc.wait_ge(sem.offv, 2)
-    for t in (1, 2, 3):
-        gather_s(t, "near", "nears")
-    v.wait_ge(sem.offv, 2)
+    for t in (2, 3):
+        sc.wait_ge(sem["off%d" % t], 1)
+        gather("s", "far", (t,))
+    sc.wait_ge(sem.off0, 1)
+    sc.wait_ge(sem.off1, 1)
+    gather("s", "near", (2, 3, 1, 0))
+    sc.wait_ge(sem.lda, 16)
+    sc.wait_ge(sem.offas, 2)
+    gather("s", "a", (2, 3))
+    gather("s", "own", (2,))
+    if side:
+        sc.wait_ge(sem.av, 2)
+        sc.wait_ge(sem["as"], 2)
+        move("s", block(BA), block(both + CI), "near")
+    gather("s", "own", (3,))
     v.wait_ge(sem.ldb, 16)
-    gather_v(0, "far", "farv")
-    gather_v(1, "far", "farv")
+    for t in (0, 1):
+        v.wait_ge(sem["off%d" % t], 1)
+        gather("v", "far", (t,))
+    v.wait_ge(sem.lista, 128)
+    offsets((2, 3), KB, KB + KA, "offas")
     v.wait_ge(sem.farv, 2)
     v.wait_ge(sem.fars, 2)
-    v.quantize_mx(T.qc[:], T.qs[:], T.tf[:]).then_inc(sem.qf, 1)
-    gather_v(0, "near", "nearv")
-    v.wait_ge(sem.lista, 128)
-    for t in (2, 3, 0, 1):
-        offsets("a", t, "offa")
-    v.wait_ge(sem.nearv, 1)
-    v.wait_ge(sem.nears, 3)
-    e = near_at(rank)
-    v.quantize_mx(T.lbc[:, e:e + PAIR], T.lbs[:, e:e + PAIR], T.tn[:]).then_inc(sem.qn, 1)
-    sc.wait_ge(sem.offa, 4)
-    sc.wait_ge(sem.lda, 16)
-    v.wait_ge(sem.offa, 4)
+    v.quantize_mx(T.lc[:, FAR:FAR + PAIR], T.ls[:, FAR:FAR + PAIR], T.tf[:]).then_inc(sem.qf, 1)
+    offsets((0, 1), KB, KB + KA, "offav")
+    gather("v", "own", (0, 1))
     v.wait_ge(sem.lda, 16)
-    gather_s(2, "a", "as")
-    gather_s(3, "a", "as")
-    gather_v(0, "a", "av")
-    gather_v(1, "a", "av")
-    v.wait_ge(sem.zeros, 1)
+    v.wait_ge(sem.offav, 2)
+    gather("v", "a", (0, 1))
     v.wait_ge(sem.av, 2)
     v.wait_ge(sem["as"], 2)
-    v.quantize_mx(T.lac[:, run:run + 128], T.las[:, run:run + 128], T.ta[:]).then_inc(sem.qa, 1)
+    move("v", block(0), block(both + CI * (1 - side)), "near")
+    v.wait_ge(sem.nearv, 1)
+    v.wait_ge(sem.nears, 4 + side)
+    v.quantize_mx(T.lc[:, MIX:MIX + mixw], T.ls[:, MIX:MIX + mixw], T.tn[:, 4 * CJ:4 * (CJ + mixw)]).then_inc(sem.qn, 1)
+    v.wait_ge(sem.ownv, 2)
+    v.wait_ge(sem.owns, 2)
+    v.wait_ge(sem.qn, 1)
+    v.quantize_mx(T.lc[:, OWN:OWN + PAIR], T.ls[:, OWN:OWN + PAIR], T.tn[:, 0:4 * PAIR]).then_inc(sem.qo, 1)
 
     n = [0]
 
@@ -321,81 +298,75 @@ def rank_program(g, core, T, topo):
 
     def settle():
         v.wait_ge(sem.vc, n[0])
-    shift = [land[q] - CI * q for q in range(N)]
-    jumps = [q for q in range(1, N) if shift[q] != shift[q - 1]]
-    v.wait_ge(sem.ldpj, 16)
-    done(v.tensor_scalar(T.pjt[:], T.pjl[:], CJ * bland(rank, 0)[1], None, A.add))
-    v.wait_ge(sem.ldpi, 128)
-    done(v.tensor_scalar(T.pit[:], T.pil[:], shift[0], None, A.add))
-    for q in jumps:
-        done(v.tensor_scalar(T.pim[:, 8 * q:8 * q + 8], T.pil[:], CI * q, shift[q] - shift[q - 1], A.is_ge, A.mult))
-    settle()
-    done(v.tensor_scalar(T.pju[:], T.pjt[:], SB - 1, None, A.bitwise_and))
-    for q in jumps:
-        done(v.tensor_tensor(T.pit[:], T.pit[:], T.pim[:, 8 * q:8 * q + 8], A.add))
-        settle()
-    done(v.tensor_copy(T.pio[:], T.pit[:]))
-    done(v.tensor_copy(T.pjo[:], T.pju[:]))
+    v.wait_ge(sem.ldpj, 128)
+    done(v.tensor_copy(T.pjo[:], T.pjl[:]))
+    steps = {}
+    for i, a0 in ((1, TILE1), (2, TILE2)):
+        f = [-999] * 128
+        for q in range(N):
+            if 0 <= aat[q] - a0 < 128:
+                f[aat[q] - a0:aat[q] - a0 + CI] = [CI * q - (aat[q] - a0)] * CI
+        jumps = [p for p in range(1, 128) if f[p] != f[p - 1]]
+        steps[i] = len(jumps) + 1
+        done(v.tensor_scalar(T.step[:, 8 * i:8 * i + 1], T.partf[:], f[0], None, A.add))
+        for j, p in enumerate(jumps):
+            done(v.tensor_scalar(T.step[:, 8 * i + 1 + j:8 * i + 2 + j], T.partf[:], p, f[p] - f[p - 1], A.is_ge, A.mult))
     settle()
     sc.wait_ge(sem.vc, n[0])
+    for i in (1, 2):
+        done(v.tensor_reduce(T.step[:, i:i + 1], T.step[:, 8 * i:8 * i + steps[i]], AxisListType.X, A.add))
     v.wait_ge(sem.filled, 1)
-    v.wait_ge(sem.cnt, 1)
-    done(v.tensor_copy(T.inv[:].indirect(T.pio[:, 0:8]), T.count[:]))
-    v.wait_ge(sem.pf, 1)
-    done(v.tensor_scalar(T.eye[:], T.count[:], T.partf[:, 0:1], None, A.is_equal))
+    v.wait_ge(sem.cast, 1)
+    done(v.tensor_tensor(T.both[:], T.piall[:], T.frac[:], A.add))
     settle()
-    for dg, (c, _) in (("dg1", view1), ("dg2", view2)):
-        done(v.tensor_tensor(T[dg][:], T.inv[:, c:c + 128], T.eye[:], A.mult))
+    for i in (1, 2):
+        done(v.tensor_scalar(T["dg%d" % i][:], T.both[:], T.step[:, i:i + 1], 256, A.subtract, A.mult))
     settle()
-    done(v.tensor_reduce(T.ix1f[:], T.dg1[:], AxisListType.X, A.add))
-    done(v.tensor_reduce(T.ix2f[:], T.dg2[:], AxisListType.X, A.add))
+    for i in (1, 2):
+        done(v.tensor_reduce(T["ix%df" % i][:], T["dg%d" % i][:], AxisListType.X, A.min, apply_absolute_value=True))
     settle()
-    if both:
-        done(v.memset(T.ix2f[0:both, :], 999.0))
-        settle()
     v.tensor_copy(T.ix1[:], T.ix1f[:]).then_inc(sem.ixd, 1)
     v.tensor_copy(T.ix2[:], T.ix2f[:]).then_inc(sem.ixd, 1)
 
-    counts = arrivals(topo, rank)
-    v0 = bland(rank, rank)[0]
-    lead = GCOL[rank] % 2 == 0
-    order = (0, 2, 1)
-    need = {0: ["arr1"] + (["arr0"] if lead else []), 2: ["arr3"] + ([] if lead else ["arr0"]), 1: ["arr2"]}
-    te.wait_ge(sem.qn, 1)
-    te.wait_ge(sem.qa, 1)
-    te.wait_ge(sem.arre, counts["arre"])
-    for i in range(6):
-        if i < 3:
-            for s in need[order[i]]:
-                te.wait_ge(sem[s], counts[s])
-        if i == 3:
-            te.wait_ge(sem.arrl, counts["arrl"])
-        a0 = (view1 if i < 3 else view2)[0]
-        b0, b1 = CHUNKS[order[i % 3]]
-        te.matmul_mx(T.ps[:, 512 * i:512 * i + b1 - b0], T.lac[:, a0:a0 + 128], T.las[:, a0:a0 + 128],
-                     T.lbc[:, v0 + b0:v0 + b1], T.lbs[:, v0 + b0:v0 + b1], True, True).then_inc(sem["m%d" % i], 1)
-    for i in (1, 2):
+    counts = arrivals(topo, core)
+    near = [(bat[xn], PAIR, [xn, rank], [], "s"), (SN - CJ, PAIR, [sn], [], "v")]
+    tiles = {1: near + [(FARB, PAIR, sf, ["far0"], "v"), (FARB + PAIR, PAIR, xf, ["far1"], "s"),
+                        (MATE - CJ, PAIR, [mate], ["mate"], "v")],
+             2: [(FARB + PAIR, PAIR + CJ, xf + [mate], [], "v"), (FARB, PAIR, sf, [], "s")] + near}
+    for s in ("qz", "qf", "qn", "qo"):
+        te.wait_ge(sem[s], 1)
+    te.wait_ge(sem.moved, 64)
+    te.wait_ge(sem.near, counts["near"])
+    m = 0
+    for i, a0 in ((1, TILE1), (2, TILE2)):
         s, y, hy = T["s%d" % i], T["y%d" % i], JW // 2
         cv, cs, yd = sem["c%dv" % i], sem["c%ds" % i], sem["yd%d" % i]
-        for k in range(3):
-            m = 3 * (i - 1) + k
-            b0, b1 = CHUNKS[order[k]]
-            src, dst = T.ps[:, 512 * m:512 * m + b1 - b0], s[:, b0:b1]
-            if k == 0:
-                sc.wait_ge(sem["m%d" % m], 1)
-                sc.activation(dst, src, COPY).then_inc(cs, 1)
-            else:
-                v.wait_ge(sem["m%d" % m], 1)
-                v.tensor_copy(dst, src).then_inc(cv, 1)
-        v.wait_ge(cv, 2)
-        v.wait_ge(cs, 1)
-        v.tensor_copy(y[:, 0:hy], s[:].indirect(T.pjo[:, 0:12])).then_inc(yd, 1)
-        sc.wait_ge(cv, 2)
-        sc.wait_ge(cs, 1)
-        sc.activation(y[:, hy:JW], s[:].indirect(T.pjo[:, 12:24]), COPY).then_inc(yd, 1)
+        copies = {"v": 0, "s": 0}
+        if i == 2:
+            te.wait_ge(sem.late, counts["late"])
+        for b0, w, qs, need, who in tiles[i]:
+            for x in need:
+                te.wait_ge(sem[x], counts[x])
+            if m == 8:
+                te.wait_ge(sem.c1s, 4)
+            bank = 512 * (m % 8)
+            te.matmul_mx(T.ps[:, bank:bank + w], T.lc[:, a0:a0 + 128], T.ls[:, a0:a0 + 128],
+                         T.lc[:, b0:b0 + w], T.ls[:, b0:b0 + w], True, True).then_inc(sem["m%d" % m], 1)
+            (sc if who == "s" else v).wait_ge(sem["m%d" % m], 1)
+            starts = [j for j in range(len(qs)) if j == 0 or qs[j] != qs[j - 1] + 1 or bat[qs[j]] != bat[qs[j - 1]] + CJ] + [len(qs)]
+            for j0, j1 in zip(starts, starts[1:]):
+                c = bank + bat[qs[j0]] - b0
+                move(who, s[:, CJ * qs[j0]:CJ * (qs[j0] + j1 - j0)], T.ps[:, c:c + CJ * (j1 - j0)], "c%d" % i)
+                copies[who] += 1
+            m += 1
+        for q in (v, sc):
+            q.wait_ge(cv, copies["v"])
+            q.wait_ge(cs, copies["s"])
+        v.tensor_copy(y[:, 0:hy], s[:].indirect(T.pjo[:, 0:hy // 16])).then_inc(yd, 1)
+        sc.activation(y[:, hy:JW], s[:].indirect(T.pjo[:, hy // 16:24]), COPY).then_inc(yd, 1)
 
     g.wait_ge(sem.ixd, 2)
-    for i, rows in ((1, view1[1]), (2, view2[1])):
+    for i, rows in ((1, 128), (2, 5 * CI)):
         g.wait_ge(sem["yd%d" % i], 2)
         g.indirect_dma_start(out=T.y[:], out_offset=IndirectOffsetOnAxis(ap=T["ix%d" % i][0:rows, 0:1], axis=0),
                              in_=T["y%d" % i][0:rows, 0:JW], in_offset=None, bounds_check=M - 1,

@@ -1,5 +1,5 @@
-from concourse.bass import DstId, RemoteDMATransfer, IndirectOffsetOnAxis
-from concourse.mybir import dt, AluOpType, AxisListType, ActivationFunctionType
+from concourse.bass import DstId, RemoteDMATransfer
+from concourse.mybir import dt, AluOpType, ActivationFunctionType
 
 CORES = [3, 11, 19, 27, 35, 43, 51, 59]
 N = 8
@@ -7,65 +7,53 @@ TA, TB, CI, CJ, JW, M = 256, 256, 24, 64, 384, 128
 SIDE = [r // 4 for r in range(N)]
 GCOL = [r % 4 for r in range(N)]
 PAIR = 2 * CJ
-SB = N * CJ
-KB, KA, KL = 16, 3, 20
 BA = CJ + CI
-SPARE = 128 - 5 * CI
+SA = N * CI
+KA, KB, KI, KJ = 3, 16, 8, 24
+LB, LA, LI, LJ = 0, 16, 20, 28
+KO = 20
 
-FAR = 0
-SN = FAR + PAIR
-TILE1 = SN + CJ
-XN = TILE1 + 128 - CI
-OWN = XN + BA
-MIX = OWN + CJ
-MIXW = BA + 3 * CI
-FARB = MIX + MIXW + SPARE
-MATE = FARB + 2 * PAIR
-TILE2 = MATE + CJ
-ZERO = TILE2 + 5 * CI
-LW = ZERO + 128
+OPT = dict(order=["aoc+axc", "aos+axs", "foc+fxc", "fos+fxs", "xnc+mtc+snc", "xns+mts+sns"], batches="mnff",
+           at={"aoc": 0, "aos": 1, "axc": 5, "axs": 6, "foc": 3, "fos": 4, "fxc": 2, "fxs": 6, "snc": 0, "sns": 1},
+           fills=[3, 0], near_v=3, tail_v="c0 c1 g0 g1 d0 d1 e0 e1 t0 t1", tail_s="c0 c1 g0 g1 s0 s1", afirst=True, one=False)
 
+NEAR = 0
+MATE = NEAR + 2 * BA
+RUN = MATE + CJ
+XN = RUN + SA - CI
+SN = XN + BA
+FARB = SN + CJ
+FAR = FARB + 2 * PAIR
+BOTH = FAR + PAIR
+LW = BOTH + 128
+
+JOBS = [x + k for x in ("ao", "ax", "fo", "fx", "sn", "xn", "mt") for k in "cs"]
 SCRATCH = {
     "wa": ("sbuf", [128, 4 * TA], "bfloat16"),
     "wb": ("sbuf", [128, 4 * TB], "bfloat16"),
-    "lists": ("sbuf", [128, KL], "int32"),
-    "off": ("sbuf", [128, 4 * KL], "uint16"),
+    "lists": ("sbuf", [128, LJ + KJ], "int32"),
+    "off": ("sbuf", [128, 4 * KO], "uint16"),
+    "ta": ("sbuf", [128, 4 * 128], "bfloat16"),
     "tf": ("sbuf", [128, 4 * PAIR], "bfloat16"),
-    "tn": ("sbuf", [128, 4 * (CJ + MIXW)], "bfloat16"),
-    "tz": ("sbuf", [128, 4 * 128], "bfloat16"),
-    "hfc": ("sbuf", [128, CJ], "float8_e4m3fn_x4"),
-    "hfs": ("sbuf", [128, CJ], "uint8"),
-    "hac": ("sbuf", [128, 2 * CI], "float8_e4m3fn_x4"),
-    "has": ("sbuf", [128, 2 * CI], "uint8"),
-    "hmc": ("sbuf", [128, BA + SPARE], "float8_e4m3fn_x4"),
+    "tn": ("sbuf", [128, 4 * 2 * BA], "bfloat16"),
     "lc": ("sbuf", [128, LW], "float8_e4m3fn_x4"),
     "ls": ("sbuf", [128, LW], "uint8"),
-    "pjl": ("sbuf", [128, 24], "int32"),
-    "pirow": ("sbuf", [128, M], "int32"),
-    "piall": ("sbuf", [128, M], "int32"),
-    "step": ("sbuf", [128, 24], "float32"),
-    "pjo": ("sbuf", [128, 24], "uint16"),
-    "partf": ("sbuf", [128, 1], "float32"),
-    "count": ("sbuf", [128, 128], "float32"),
-    "frac": ("sbuf", [128, 128], "float32"),
-    "both": ("sbuf", [128, 128], "float32"),
-    "dg1": ("sbuf", [128, 128], "float32"),
-    "dg2": ("sbuf", [128, 128], "float32"),
-    "ix1f": ("sbuf", [128, 1], "float32"),
-    "ix2f": ("sbuf", [128, 1], "float32"),
-    "ix1": ("sbuf", [128, 1], "int32"),
-    "ix2": ("sbuf", [128, 1], "int32"),
-    "s1": ("sbuf", [128, SB], "float32"),
-    "s2": ("sbuf", [128, SB], "float32"),
-    "y1": ("sbuf", [128, JW], "float32"),
-    "y2": ("sbuf", [128, JW], "float32"),
-    "ps": ("psum", [128, 8 * 512], "float32"),
+    "quarter": ("sbuf", [128, 1], "float32"),
+    "wi": ("sbuf", [128, 10 * KI], "int32"),
+    "wj": ("sbuf", [128, 20 * KJ], "int32"),
+    "pio": ("sbuf", [128, 4 * KI], "uint16"),
+    "pjo": ("sbuf", [128, KJ], "uint16"),
+    "prod": ("sbuf", [128, 4 * SA], "float32"),
+    "got": ("sbuf", [128, 512], "float32"),
+    "put": ("sbuf", [128, 512], "float32"),
+    "rows": ("sbuf", [128, 512], "float32"),
+    "yy": ("sbuf", [128, JW], "float32"),
+    "ps": ("psum", [128, 4 * 512], "float32"),
 }
-SEMAPHORES = ["listb", "lista", "spread", "ldb", "lda", "ldpi", "ldpj", "cnt", "filled", "zeros", "cast",
-              "off0", "off1", "off2", "off3", "offas", "offav", "fars", "farv", "nears", "nearv", "as", "av", "owns", "ownv",
-              "qz", "qf", "qn", "qo", "vc", "ixd", "go", "moved", "hfc", "hfs", "hac", "has", "hmc",
-              "mate", "near", "far0", "far1", "late", "sent",
-              "m0", "m1", "m2", "m3", "m4", "m5", "m6", "m7", "m8", "c1v", "c1s", "c2v", "c2s", "yd1", "yd2", "ystored"]
+SCRATCH.update({"h" + j: ("sbuf", [128, BA + 8], "float8_e4m3fn_x4" if j[-1] == "c" else "uint8") for j in JOBS})
+SEMAPHORES = (["ls", "lp", "lda", "ldb", "zeros", "sp", "ov", "os", "av", "as", "fv", "fs", "nv", "ns", "moved",
+               "qa", "qf", "qn", "ii", "jj", "run", "wf", "wm", "wn", "sent", "m0", "m1", "m2", "m3", "tv", "yv", "ys", "stored"]
+              + ["G0", "G1", "G2", "G3", "P1", "P2", "P3"] + JOBS + [x + h + e for x in "cgmh" for h in "01" for e in "vs"])
 
 
 def groups(topo, q):
@@ -73,70 +61,68 @@ def groups(topo, q):
     mate = [d for d in range(N) if topo.mates(chip[q], chip[d])][0]
     same = [d for d in range(N) if d != q and topo.same_plane(chip[q], chip[d])]
     cross = [d for d in range(N) if d not in same + [q, mate]]
-    near = lambda ds: [d for d in ds if GCOL[d] // 2 == GCOL[q] // 2]
-    far = lambda ds: [d for d in ds if GCOL[d] // 2 != GCOL[q] // 2]
-    return mate, near(same)[0], far(same), near(cross)[0], far(cross)
-
-
-def sides_at(q):
-    return BA + CI * SIDE[q]
+    sn, xn = [d for d in same if GCOL[d] == GCOL[q]][0], [d for d in cross if GCOL[d] == GCOL[mate]][0]
+    return mate, sn, [d for d in same if d != sn], xn, [d for d in cross if d != xn]
 
 
 def places(topo, d):
     mate, sn, sf, xn, xf = groups(topo, d)
-    far = sorted(sf + xf)
-    b = {sn: SN, xn: XN + CI, d: OWN, mate: MATE}
-    a = {sn: TILE1, d: TILE1 + CI, xn: XN, mate: TILE2}
+    order = [mate] + [q % N for q in range(mate, mate + N) if q % N not in (mate, xn)] + [xn]
+    a = {q: RUN + CI * i for i, q in enumerate(order)}
+    b = {d: MATE - CJ, mate: MATE, xn: XN + CI, sn: SN}
     b.update({q: FARB + CJ * i for i, q in enumerate(sf + xf)})
-    a.update({q: TILE2 + CI + CI * i for i, q in enumerate(far)})
-    return b, a
+    return a, b
+
+
+def jobs(topo, q):
+    mate, sn, sf, xn, xf = groups(topo, q)
+    fcol = lambda ds: FAR + CJ * sorted([GCOL[sf[0]], GCOL[xf[0]]]).index(GCOL[ds[0]])
+    a = lambda ds: (BOTH, 2 * CI, [(d, CI * SIDE[d], CI, places(topo, d)[0][q], "run") for d in ds])
+    f = lambda ds: (fcol(ds), CJ, [(d, 0, CJ, places(topo, d)[1][q], "wf") for d in ds])
+    return {"ao": a(sf + [sn]), "ax": a(xf), "fo": f(sf), "fx": f(xf), "sn": (NEAR + BA, BA, [(sn, CI, CJ, SN, "wn")]),
+            "xn": (NEAR, BA, [(xn, 0, BA, XN, "wn")]), "mt": (NEAR + CI, BA, [(mate, 0, BA, MATE, "wm")])}
+
+
+def split(topo, src, ready, parts):
+    width = lambda t: t[2] * (4 if t[3][-1] == "c" else 1)
+    cs = []
+    for w in sorted({width(t) for t in parts}, reverse=True):
+        off = [t for t in parts if width(t) == w and topo.chip(t[0]) != topo.chip(src)]
+        on = [t for t in parts if width(t) == w and t not in off]
+        more = [off[i:i + 2] for i in range(0, len(off), 2)] or [[]]
+        more[0] += on
+        cs += more
+    return [(ready if i == 0 else [], c) for i, c in enumerate(cs)]
 
 
 def plan(topo, q):
-    me = CORES[q]
-    mate, sn, sf, xn, xf = groups(topo, q)
-    others = [c for c in topo.cores_of(me) if c != me]
-    here = lambda cs: sorted(cs, key=lambda c: topo.die(c) != topo.die(me))
-    x1, x2, x3 = here([c for c in others if topo.may_write(c, CORES[mate])])[:3]
-    p = here([c for c in others if not topo.may_write(c, CORES[mate])])
-    s2, s1 = p[0], p[-1]
-    fcol = lambda ds: FAR + CJ * (GCOL[ds[0]] % 2)
-    both = MIX + sides_at(q)
-
-    def far(k, ds):
-        return [(CORES[d], "far%d" % (ds == xf), CJ, "hf" + k, 0, "l" + k, places(topo, d)[0][q]) for d in ds]
-
-    def late(k, ds):
-        return [(CORES[d], "late", CI, "ha" + k, CI * SIDE[d], "l" + k, places(topo, d)[1][q]) for d in ds]
-
-    def near(k):
-        return [(CORES[sn], "near", BA, "l" + k, OWN, "l" + k, SN), (CORES[xn], "near", BA, "l" + k, MIX, "l" + k, XN)]
-
-    def last(k):
-        return [(CORES[mate], "mate", BA, "l" + k, MIX + CI, "l" + k, MATE)]
-
-    def hop(buf, w, to):
-        return [(c, buf, w, "l" + buf[-1], col, buf, 0) for c, col in to]
-    return {me: [("qf", hop("hfc", CJ, [(x2, fcol(xf)), (s2, fcol(sf))])),
-                 (None, hop("hfs", CJ, [(x1, fcol(xf)), (s1, fcol(sf))])),
-                 ("qn", []),
-                 ("beside", hop("hac", 2 * CI, [(x3, both), (s1, both)])),
-                 ("qo", near("c") + hop("hmc", BA, [(x1, MIX + CI)])),
-                 ("beside", hop("has", 2 * CI, [(x2, both), (s2, both)])),
-                 (None, near("s")), ("go", last("s"))],
-            x1: [("hfs", far("s", xf)), ("hmc", [(CORES[mate], "mate", BA, "hmc", 0, "lc", MATE)])],
-            x2: [("hfc", far("c", xf)), ("has", late("s", xf))],
-            x3: [("hac", late("c", xf))],
-            s2: [("hfc", far("c", sf)), ("has", late("s", sf))],
-            s1: [("hfs", far("s", sf)), ("hac", late("c", sf))]}
+    me, what = CORES[q], jobs(topo, q)
+    helpers = sorted([c for c in topo.cores_of(me) if c != me], key=lambda c: topo.die(c) != topo.die(me))
+    calls, seen = {me: []}, []
+    for entry in OPT["order"]:
+        tiles = sorted({"q" + {"a": "a", "f": "f"}.get(j[0], "n") for j in entry.split("+")})
+        ready = [x for x in tiles if x not in seen]
+        seen += tiles
+        tr = []
+        for job in entry.split("+"):
+            col, w, to = what[job[:2]]
+            own = "l" + job[2]
+            out = lambda buf, c: [(CORES[d], s, n, buf, c + o, own, at) for d, o, n, at, s in to]
+            if job in OPT["at"]:
+                h = helpers[OPT["at"][job]]
+                tr.append((h, job, w, own, col, "h" + job, 0))
+                calls.setdefault(h, []).extend(split(topo, h, [job], out("h" + job, 0)))
+            else:
+                tr += out(own, col)
+        calls[me] += split(topo, me, ready, tr)
+    return calls
 
 
-def masks(topo, src, parts, beside=False):
+def masks(topo, src, parts):
     off = [i for i, x in enumerate(parts) if topo.chip(x[0]) != topo.chip(src)]
     on = [i for i in range(len(parts)) if i not in off]
-    plane = [c for c in CORES if topo.same_plane(topo.chip(c), topo.chip(src))]
-    eoff = topo.engines(src, plane[0]) if off or beside in ("beside", "below") else []
-    eon = [e for e in topo.engines(src, parts[on[0]][0]) if (e in eoff) == (beside == "below")] if on else []
+    eoff = topo.engines(src, parts[off[0]][0]) if off else []
+    eon = [e for e in topo.engines(src, parts[on[0]][0]) if e not in eoff] if on else []
     share = {i: e[k::len(xs)] for xs, e in ((off, eoff), (on, eon)) for k, i in enumerate(xs)}
     return [sum(1 << e for e in share[i]) for i in range(len(parts))]
 
@@ -154,7 +140,7 @@ def arrivals(topo, core):
     for q in range(N):
         for c, calls in plan(topo, q).items():
             for ready, parts in calls:
-                for x, m in zip(parts, masks(topo, c, parts, ready) if parts else []):
+                for x, m in zip(parts, masks(topo, c, parts)):
                     if x[0] == core:
                         n[x[1]] = n.get(x[1], 0) + engines_in(m)
     return n
@@ -163,213 +149,230 @@ def arrivals(topo, core):
 def remote_calls(g, core, T, topo, q):
     counts, used = arrivals(topo, core), 0
     for ready, parts in plan(topo, q).get(core, []):
-        if ready == "go":
-            g.sem_inc(T.sem.go, 1)
-        elif ready and ready not in ("beside", "below"):
-            g.wait_ge(T.sem[ready], counts.get(ready, 1))
-        if not parts:
-            continue
+        for s in ready:
+            g.wait_ge(T.sem[s], counts.get(s, 1))
         tr = []
-        for (c, sem, w, s, sc, d, dc), m in zip(parts, masks(topo, core, parts, ready)):
+        for (c, sem, w, s, sc, d, dc), m in zip(parts, masks(topo, core, parts)):
             rid, pid, _ = topo.addr(c)
             tr.append(RemoteDMATransfer(dst_ids=[DstId(rid=rid, pnc=pid)], dma_engine_mask=m, remote_sem=T.sem[sem],
                                         srcs=[view(T, s, sc, w)], dsts=[view(T, d, dc, w)], alu_op=0))
             used += engines_in(m)
         g.remote_dma_fused(tr, local_sem=T.sem.sent)
-    return used
+    if used:
+        g.wait_ge(T.sem.sent, used)
 
 
 def rank_program(g, core, T, topo):
     rank = T.rank_of(core)
+    for q in range(N):
+        if topo.chip(CORES[q]) == topo.chip(core):
+            remote_calls(g, core, T, topo, q)
     if rank is None:
-        q = [r for r in range(N) if topo.chip(CORES[r]) == topo.chip(core)]
-        used = remote_calls(g, core, T, topo, q[0]) if q else 0
-        if used:
-            g.wait_ge(T.sem.sent, used)
         return
     v, sc, sy, te, sem = g.vector, g.scalar, g.sync, g.tensor, T.sem
     COPY, A = ActivationFunctionType.Copy, AluOpType
     mate, sn, sf, xn, xf = groups(topo, rank)
-    far = sorted(sf + xf)
-    bat, aat = places(topo, rank)
-    side, both = SIDE[rank], sides_at(rank)
-    mixw = both + 2 * CI
+    aat, bat = places(topo, rank)
+    starts = {"m": [MATE - CJ], "n": [XN + CI], "f": [FARB, FARB + PAIR]}
+    wins = [(x, starts[x].pop(0)) for x in OPT["batches"]]
+    side = SIDE[rank]
+    eng = {"v": v, "s": sc}
 
-    for k in range(2):
-        (sy, sc)[k].dma_start(T.lists[16 * k:16 * k + 16, 0:KB], T.sb[:]).then_inc(sem.listb, 16)
-    sy.dma_start(T.wb[:], T.b[:]).then_inc(sem.ldb, 16)
-    for k in range(8):
-        (sy, sc)[k % 2].dma_start(T.lists[16 * k:16 * k + 16, KB:KB + KA], T.sa[:]).then_inc(sem.lista, 16)
-    sc.dma_start(T.wa[:], T.a[:]).then_inc(sem.lda, 16)
-    for k in range(8):
-        sy.dma_start(T.pjl[16 * k:16 * k + 16, :], T.pj[:]).then_inc(sem.ldpj, 16)
-
-    g.iota(T.partf[:], [[1, 1]], 0, 1, allow_small_or_imprecise_dtypes=True).then_inc(sem.cnt, 1)
-    g.iota(T.count[:], [[1, 16], [16, 8]], 0, 0, allow_small_or_imprecise_dtypes=True).then_inc(sem.cnt, 1)
-    g.dma_start(T.pirow[0:1, :], T.pi[:]).then_inc(sem.ldpi, 16)
-    used = remote_calls(g, core, T, topo, rank)
-    g.wait_ge(sem.ldpi, 16)
-    g.partition_broadcast(T.piall[:], T.pirow[0:1, :], 128).then_inc(sem.cast, 1)
-
-    sy.wait_ge(sem.qz, 1)
+    def lists(q, k, c, t, s):
+        q.dma_start(T.lists[16 * k:16 * k + 16, c:c + t.shape[1]], t[:]).then_inc(sem[s], 16)
+    for c, t in ((LA, T.sa), (LB, T.sb)):
+        lists(sy, 0, c, t, "ls")
+        lists(sc, 1, c, t, "ls")
+    for x in ("ab" if OPT["afirst"] else "ba"):
+        sy.dma_start(T["w" + x][:], T[x][:]).then_inc(sem["ld" + x], 16)
+    for c, t in ((LI, T.pi), (LJ, T.pj)):
+        lists(sc, 0, c, t, "lp")
+        lists(sc, 1, c, t, "lp")
+    sy.wait_ge(sem.qa, 1)
     for name in ("lc", "ls"):
-        sy.dma_start(view(T, name, TILE1 + 2 * CI, 128 - 3 * CI), view(T, name, ZERO, 128 - 3 * CI)).then_inc(sem.moved, 16)
-    sy.wait_ge(sem.qn, 1)
-    sy.wait_ge(sem.go, 1)
-    for name in ("lc", "ls"):
-        sy.dma_start(view(T, name, TILE1 + CI, CI), view(T, name, MIX + BA, CI)).then_inc(sem.moved, 16)
+        sy.dma_start(view(T, name, aat[rank], CI), view(T, name, BOTH + CI * side, CI)).then_inc(sem.moved, 16)
 
-    v.memset(T.tz[:], 0.0).then_inc(sem.zeros, 1)
-    v.wait_ge(sem.zeros, 1)
-    v.quantize_mx(T.lc[:, ZERO:LW], T.ls[:, ZERO:LW], T.tz[:]).then_inc(sem.qz, 1)
-    v.wait_ge(sem.cnt, 2)
-    v.tensor_scalar(T.frac[:], T.count[:], 1.0 / 256, None, A.mult).then_inc(sem.filled, 1)
+    n = {}
 
-    pieces = {"far": (T.tf, 0, T.wb, 8 - 8 * (GCOL[rank] // 2), 8), "own": (T.tn, 0, T.wb, 4 * GCOL[rank], 4),
-              "near": (T.tn, BA, T.wb, 4 * GCOL[mate], 4), "a": (T.tn, CJ + both, T.wa, KB, KA)}
+    def inc(ins, s):
+        ins.then_inc(sem[s], 1)
+        n[s] = n.get(s, 0) + 1
 
-    def offsets(ts, k0, k1, s):
-        for t in ts:
-            v.tensor_scalar(T.off[:, KL * t + k0:KL * t + k1], T.lists[:, k0:k1], 4, t, A.mult, A.add).then_inc(sem[s], 1)
+    def wait(e, *ss):
+        for s in ss:
+            e.wait_ge(sem[s], n[s])
 
     def move(who, o, i, s):
-        (v.tensor_copy(o, i) if who == "v" else sc.activation(o, i, COPY)).then_inc(sem[s + who], 1)
+        inc(v.tensor_copy(o, i) if who == "v" else sc.activation(o, i, COPY), s + who)
 
-    def gather(who, what, ts):
-        tile, c, win, k, n = pieces[what]
+    wi = lambda j, w=1, p=0: T.wi[p:p + 32, KI * j:KI * (j + w)]
+    wj = lambda j, w=1: T.wj[:, KJ * j:KJ * (j + w)]
+    pi, pj = T.lists[0:32, LI:LI + KI], T.lists[:, LJ:LJ + KJ]
+    d = [aat[r] - RUN - CI * r for r in range(N)]
+    jumps = ([r for r in range(1, N) if d[r] != d[r - 1]] + [0, 0, 0])[:3]
+    k_of = {r: [i for i, (x, c) in enumerate(wins) if c <= bat[r] < c + PAIR][0] for r in range(N)}
+    e = [512 - 4 * (bat[r] - wins[k_of[r]][1]) + 32 * k_of[r] - CJ * r for r in range(N)]
+    ts, tt, tc = v.tensor_scalar, v.tensor_tensor, v.tensor_copy
+    nk = 4 if OPT["one"] else 2
+    chain_i = [[(ts, wi(0), pi, d[0], None, A.add)]
+               + [(ts, wi(1 + j), pi, CI * r, d[r] - d[r - 1] if r else 0, A.is_ge, A.mult) for j, r in enumerate(jumps)],
+               [(tt, wi(4, 2), wi(0, 2), wi(2, 2), A.add)],
+               [(tt, wi(6), wi(4), wi(5), A.add), (tt, wi(7), wi(4), wi(5), A.add)],
+               [(tc, wi(8, 1, 32 * a), T.wi[0:32, 6 * KI + 2 * a:7 * KI + 2 * a]) for a in range(4)],
+               [(ts, T.pio[:, 2 * k + h:KI * nk:2 * nk], T.wi[:, 8 * KI + h:9 * KI:2], SA * k, None, A.add) for k in range(nk) for h in range(2)]]
+    chain_j = [[(tc, T.lists[p:p + 32, LJ:LJ + KJ], T.lists[0:32, LJ:LJ + KJ]) for p in (32, 64, 96)],
+               [(ts, wj(16), pj, 32, None, A.bitwise_and), (ts, wj(0), pj, T.quarter[:, 0:1], None, A.add)]
+               + [(ts, wj(r), pj, CJ * r, e[r] - e[r - 1], A.is_ge, A.mult) for r in range(1, N)],
+               [(ts, wj(17), wj(16), -5, None, A.mult), (tt, wj(8, 4), wj(0, 4), wj(4, 4), A.add)],
+               [(tt, wj(12, 2), wj(8, 2), wj(10, 2), A.add)], [(tt, wj(14), wj(12), wj(13), A.add)],
+               [(tt, wj(15), wj(14), wj(17), A.add)], [(ts, wj(18), wj(15), 511, None, A.bitwise_and)], [(tc, T.pjo[:], wj(18))]]
+    todo = []
+    for tok in "j0 i0 j1 i1 j2 i2 j3 i3 j4 i4 j5 j6 j7".split():
+        todo += [(2 * tok[0], i == 0, op) for i, op in enumerate((chain_i if tok[0] == "i" else chain_j)[int(tok[1])])]
+
+    def fill(k):
+        for s, new, op in todo[:k]:
+            if s not in n:
+                v.wait_ge(sem.lp, 64)
+            elif new:
+                wait(v, s)
+            inc(op[0](*op[1:]), s)
+        del todo[:k]
+
+    pieces = {"a": (T.ta, 0, T.wa, LA, KA, "a"), "f": (T.tf, 0, T.wb, 4 * min(GCOL[sf[0]], GCOL[xf[0]]), 8, "f"),
+              "m": (T.tn, CI, T.wb, 4 * GCOL[mate], 4, "n"), "o": (T.tn, BA + CI, T.wb, 4 * GCOL[rank], 4, "n")}
+
+    def gather(x, who, ts):
+        tl, c, win, k, w, s = pieces[x]
         for t in ts:
-            move(who, tile[:, 4 * c + t:4 * (c + 16 * n):4], win[:].indirect(T.off[:, KL * t + k:KL * t + k + n]), what)
+            move(who, tl[:, 4 * c + t:4 * (c + 16 * w):4], win[:].indirect(T.off[:, KO * t + k:KO * t + k + w]), s)
 
-    def block(c):
-        return T.tn[:, 4 * (CJ + c):4 * (CJ + c + CI)]
+    def quantise(x, tl, at, w):
+        wait(v, x + "v", x + "s")
+        inc(v.quantize_mx(T.lc[:, at:at + w], T.ls[:, at:at + w], tl[:]), "q" + x)
 
-    v.wait_ge(sem.listb, 32)
+    def both(x):
+        for who in "sv":
+            wait(eng[who], "ov", "os")
+            eng[who].wait_ge(sem["ld" + x.replace("f", "b")], 16)
+            gather(x, who, (2, 3) if who == "s" else (0, 1))
+
+    def beside():
+        wait(sc, "av", "as")
+        for c, s in ((0, 1 - side), (BA, side)):
+            move("s", T.tn[:, 4 * c:4 * (c + CI)], T.ta[:, 4 * CI * s:4 * CI * (s + 1)], "n")
+    inc(v.memset(T.ta[:, 8 * CI:], 0.0), "zeros")
+    for b in range(4):
+        inc(v.memset(T.quarter[32 * b:32 * b + 32, :], float(128 * b + e[0])), "zeros")
+    wait(v, "zeros")
+    v.wait_ge(sem.ls, 64)
     for p in (32, 64, 96):
-        v.tensor_copy(T.lists[p:p + 32, 0:KB], T.lists[0:32, 0:KB]).then_inc(sem.spread, 1)
-    v.wait_ge(sem.spread, 3)
+        inc(v.tensor_copy(T.lists[p:p + 32, 0:KB + KA], T.lists[0:32, 0:KB + KA]), "sp")
+    wait(v, "sp")
     for t in (2, 0, 3, 1):
-        offsets((t,), 0, KB, "off%d" % t)
-    sc.wait_ge(sem.ldb, 16)
-    for t in (2, 3):
-        sc.wait_ge(sem["off%d" % t], 1)
-        gather("s", "far", (t,))
-    sc.wait_ge(sem.off0, 1)
-    sc.wait_ge(sem.off1, 1)
-    gather("s", "near", (2, 3, 1, 0))
-    sc.wait_ge(sem.lda, 16)
-    sc.wait_ge(sem.offas, 2)
-    gather("s", "a", (2, 3))
-    gather("s", "own", (2,))
-    if side:
-        sc.wait_ge(sem.av, 2)
-        sc.wait_ge(sem["as"], 2)
-        move("s", block(BA), block(both + CI), "near")
-    gather("s", "own", (3,))
-    v.wait_ge(sem.ldb, 16)
-    for t in (0, 1):
-        v.wait_ge(sem["off%d" % t], 1)
-        gather("v", "far", (t,))
-    v.wait_ge(sem.lista, 128)
-    offsets((2, 3), KB, KB + KA, "offas")
-    v.wait_ge(sem.farv, 2)
-    v.wait_ge(sem.fars, 2)
-    v.quantize_mx(T.lc[:, FAR:FAR + PAIR], T.ls[:, FAR:FAR + PAIR], T.tf[:]).then_inc(sem.qf, 1)
-    offsets((0, 1), KB, KB + KA, "offav")
-    gather("v", "own", (0, 1))
-    v.wait_ge(sem.lda, 16)
-    v.wait_ge(sem.offav, 2)
-    gather("v", "a", (0, 1))
-    v.wait_ge(sem.av, 2)
-    v.wait_ge(sem["as"], 2)
-    move("v", block(0), block(both + CI * (1 - side)), "near")
-    v.wait_ge(sem.nearv, 1)
-    v.wait_ge(sem.nears, 4 + side)
-    v.quantize_mx(T.lc[:, MIX:MIX + mixw], T.ls[:, MIX:MIX + mixw], T.tn[:, 4 * CJ:4 * (CJ + mixw)]).then_inc(sem.qn, 1)
-    v.wait_ge(sem.ownv, 2)
-    v.wait_ge(sem.owns, 2)
-    v.wait_ge(sem.qn, 1)
-    v.quantize_mx(T.lc[:, OWN:OWN + PAIR], T.ls[:, OWN:OWN + PAIR], T.tn[:, 0:4 * PAIR]).then_inc(sem.qo, 1)
-
-    n = [0]
-
-    def done(ins):
-        ins.then_inc(sem.vc, 1)
-        n[0] += 1
-
-    def settle():
-        v.wait_ge(sem.vc, n[0])
-    v.wait_ge(sem.ldpj, 128)
-    done(v.tensor_copy(T.pjo[:], T.pjl[:]))
-    steps = {}
-    for i, a0 in ((1, TILE1), (2, TILE2)):
-        f = [-999] * 128
-        for q in range(N):
-            if 0 <= aat[q] - a0 < 128:
-                f[aat[q] - a0:aat[q] - a0 + CI] = [CI * q - (aat[q] - a0)] * CI
-        jumps = [p for p in range(1, 128) if f[p] != f[p - 1]]
-        steps[i] = len(jumps) + 1
-        done(v.tensor_scalar(T.step[:, 8 * i:8 * i + 1], T.partf[:], f[0], None, A.add))
-        for j, p in enumerate(jumps):
-            done(v.tensor_scalar(T.step[:, 8 * i + 1 + j:8 * i + 2 + j], T.partf[:], p, f[p] - f[p - 1], A.is_ge, A.mult))
-    settle()
-    sc.wait_ge(sem.vc, n[0])
-    for i in (1, 2):
-        done(v.tensor_reduce(T.step[:, i:i + 1], T.step[:, 8 * i:8 * i + steps[i]], AxisListType.X, A.add))
-    v.wait_ge(sem.filled, 1)
-    v.wait_ge(sem.cast, 1)
-    done(v.tensor_tensor(T.both[:], T.piall[:], T.frac[:], A.add))
-    settle()
-    for i in (1, 2):
-        done(v.tensor_scalar(T["dg%d" % i][:], T.both[:], T.step[:, i:i + 1], 256, A.subtract, A.mult))
-    settle()
-    for i in (1, 2):
-        done(v.tensor_reduce(T["ix%df" % i][:], T["dg%d" % i][:], AxisListType.X, A.min, apply_absolute_value=True))
-    settle()
-    v.tensor_copy(T.ix1[:], T.ix1f[:]).then_inc(sem.ixd, 1)
-    v.tensor_copy(T.ix2[:], T.ix2f[:]).then_inc(sem.ixd, 1)
+        inc(v.tensor_scalar(T.off[:, KO * t:KO * t + KB + KA], T.lists[:, 0:KB + KA], 4, t, A.mult, A.add), "o" + "vs"[t // 2])
+    nv = OPT["near_v"]
+    if OPT["afirst"]:
+        both("a")
+        beside()
+        quantise("a", T.ta, BOTH, 128)
+        both("f")
+        gather("m", "s", range(4))
+        gather("o", "s", range(nv, 4))
+        fill(OPT["fills"][0])
+        quantise("f", T.tf, FAR, PAIR)
+        gather("o", "v", range(nv))
+    else:
+        both("f")
+        gather("m", "s", range(2))
+        quantise("f", T.tf, FAR, PAIR)
+        gather("o", "v", range(1))
+        both("a")
+        gather("m", "s", range(2, 4))
+        beside()
+        gather("o", "v", range(1, 2))
+        quantise("a", T.ta, BOTH, 128)
+        gather("o", "v", range(2, 4))
+    fill(OPT["fills"][1])
+    quantise("n", T.tn, NEAR, 2 * BA)
+    fill(len(todo))
 
     counts = arrivals(topo, core)
-    near = [(bat[xn], PAIR, [xn, rank], [], "s"), (SN - CJ, PAIR, [sn], [], "v")]
-    tiles = {1: near + [(FARB, PAIR, sf, ["far0"], "v"), (FARB + PAIR, PAIR, xf, ["far1"], "s"),
-                        (MATE - CJ, PAIR, [mate], ["mate"], "v")],
-             2: [(FARB + PAIR, PAIR + CJ, xf + [mate], [], "v"), (FARB, PAIR, sf, [], "s")] + near}
-    for s in ("qz", "qf", "qn", "qo"):
+    for s in ("qa", "qf", "qn"):
         te.wait_ge(sem[s], 1)
-    te.wait_ge(sem.moved, 64)
-    te.wait_ge(sem.near, counts["near"])
-    m = 0
-    for i, a0 in ((1, TILE1), (2, TILE2)):
-        s, y, hy = T["s%d" % i], T["y%d" % i], JW // 2
-        cv, cs, yd = sem["c%dv" % i], sem["c%ds" % i], sem["yd%d" % i]
-        copies = {"v": 0, "s": 0}
-        if i == 2:
-            te.wait_ge(sem.late, counts["late"])
-        for b0, w, qs, need, who in tiles[i]:
-            for x in need:
-                te.wait_ge(sem[x], counts[x])
-            if m == 8:
-                te.wait_ge(sem.c1s, 4)
-            bank = 512 * (m % 8)
-            te.matmul_mx(T.ps[:, bank:bank + w], T.lc[:, a0:a0 + 128], T.ls[:, a0:a0 + 128],
-                         T.lc[:, b0:b0 + w], T.ls[:, b0:b0 + w], True, True).then_inc(sem["m%d" % m], 1)
-            (sc if who == "s" else v).wait_ge(sem["m%d" % m], 1)
-            starts = [j for j in range(len(qs)) if j == 0 or qs[j] != qs[j - 1] + 1 or bat[qs[j]] != bat[qs[j - 1]] + CJ] + [len(qs)]
-            for j0, j1 in zip(starts, starts[1:]):
-                c = bank + bat[qs[j0]] - b0
-                move(who, s[:, CJ * qs[j0]:CJ * (qs[j0] + j1 - j0)], T.ps[:, c:c + CJ * (j1 - j0)], "c%d" % i)
-                copies[who] += 1
-            m += 1
-        for q in (v, sc):
-            q.wait_ge(cv, copies["v"])
-            q.wait_ge(cs, copies["s"])
-        v.tensor_copy(y[:, 0:hy], s[:].indirect(T.pjo[:, 0:hy // 16])).then_inc(yd, 1)
-        sc.activation(y[:, hy:JW], s[:].indirect(T.pjo[:, hy // 16:24]), COPY).then_inc(yd, 1)
+    te.wait_ge(sem.moved, 32)
+    for s in ("run", "wm", "wn"):
+        te.wait_ge(sem[s], counts[s])
+    for k, (x, c) in enumerate(wins):
+        te.wait_ge(sem["w" + x], counts["w" + x])
+        te.matmul_mx(T.ps[:, 512 * k:512 * k + SA], T.lc[:, c:c + PAIR], T.ls[:, c:c + PAIR],
+                     T.lc[:, RUN:RUN + SA], T.ls[:, RUN:RUN + SA], True, True).then_inc(sem["m%d" % k], 1)
 
-    g.wait_ge(sem.ixd, 2)
-    for i, rows in ((1, 128), (2, 5 * CI)):
-        g.wait_ge(sem["yd%d" % i], 2)
-        g.indirect_dma_start(out=T.y[:], out_offset=IndirectOffsetOnAxis(ap=T["ix%d" % i][0:rows, 0:1], axis=0),
-                             in_=T["y%d" % i][0:rows, 0:JW], in_offset=None, bounds_check=M - 1,
-                             oob_is_err=False).then_inc(sem.ystored, 16)
-    g.wait_ge(sem.sent, used)
-    g.wait_ge(sem.ystored, 32)
+    def blk(buf, h, r, p=0, w=128):
+        return buf[p:p + w, 256 * h + 64 * r:256 * h + 64 * r + 64]
+
+    def stage(who, what, h):
+        en, H = eng[who], str(h)
+        if what == "c":
+            k = 2 * h + (who == "s")
+            en.wait_ge(sem["m%d" % k], 1)
+            move(who, T.prod[:, SA * k:SA * k + SA], T.ps[:, 512 * k:512 * k + SA], "c" + H)
+        if what == "g":
+            r0, r1 = (0, 3) if who == "s" else (3, 4)
+            wait(en, "ii")
+            en.wait_ge(sem["c" + H + "v"], 1)
+            en.wait_ge(sem["c" + H + "s"], 1)
+            move(who, T.got[:, 256 * h + 64 * r0:256 * h + 64 * r1],
+                 T.prod[:, 2 * SA * h:2 * SA * (h + 1)].indirect(T.pio[:, 4 * r0:4 * r1]), "g" + H)
+
+        def turn(buf, r, shift, w):
+            for p in range(0, 128, w):
+                to = (p + shift) % 128
+                inc(v.transpose(T.rows[to:to + w, 128 * r + 64 * h:128 * r + 64 * h + 64], blk(buf, h, r, p, w)), "tv")
+        if what == "s":
+            en.wait_ge(sem["g" + H + "s"], 1)
+            for p in range(0, 128, 32):
+                move(who, blk(T.put, h, 1, (p + 32) % 128, 32), blk(T.got, h, 1, p, 32), "m" + H)
+        if what == "d":
+            v.wait_ge(sem["g" + H + "v"], 1)
+            turn(T.got, 3, 96, 32)
+        if what == "e":
+            v.wait_ge(sem["g" + H + "s"], 1)
+            turn(T.got, 0, 0, 128)
+            turn(T.got, 2, 64, 64)
+        if what == "t":
+            v.wait_ge(sem["m" + H + "s"], 4)
+            turn(T.put, 1, 0, 128)
+    def whole(who, what, r):
+        en, R = eng[who], str(r)
+        quad = lambda buf, p=0, w=128: buf[p:p + w, 128 * r:128 * r + 128]
+        copy = v.tensor_copy if who == "v" else lambda o, i: sc.activation(o, i, COPY)
+        w = 64 if r == 2 else 32
+        if what == "c":
+            en.wait_ge(sem["m" + R], 1)
+            inc(copy(T.prod[:, SA * r:SA * r + SA], T.ps[:, 512 * r:512 * r + SA]), "c0v")
+        if what == "g":
+            wait(en, "ii")
+            en.wait_ge(sem.c0v, 4)
+            inc(copy(quad(T.got), T.prod[:].indirect(T.pio[:, 8 * r:8 * r + 8])), "G" + R)
+        if what == "s":
+            en.wait_ge(sem["G" + R], 1)
+            for p in range(0, 128, w):
+                inc(copy(quad(T.put, (p + 32 * r) % 128, w), quad(T.got, p, w)), "P" + R)
+        if what == "d":
+            en.wait_ge(sem["G" + R], 1)
+            for p in range(0, 128, w):
+                inc(v.transpose(quad(T.rows, (p + 32 * r) % 128, w), quad(T.got, p, w)), "tv")
+        if what == "t":
+            v.wait_ge(sem["P" + R if r else "G0"], (1, 4, 2, 4)[r])
+            inc(v.transpose(quad(T.rows), quad(T.put if r else T.got)), "tv")
+    for who in "vs":
+        for tok in OPT["tail_" + who].split():
+            (whole if OPT["one"] else stage)(who, tok[0], int(tok[1]))
+    hy = JW // 2
+    for who, c in (("v", 0), ("s", hy)):
+        wait(eng[who], "jj", "tv")
+        move(who, T.yy[:, c:c + hy], T.rows[:].indirect(T.pjo[:, c // 16:(c + hy) // 16]), "y")
+    wait(sy, "yv", "ys")
+    sy.dma_start(T.y[:], T.yy[:]).then_inc(sem.stored, 16)
+    sy.wait_ge(sem.stored, 16)

from concourse.bass import DstId, RemoteDMATransfer
from concourse.mybir import dt, AluOpType, ActivationFunctionType

CORES = [3, 11, 19, 27, 35, 43, 51, 59]
N = 8
TA, TB, CI, CJ, JW, M = 256, 256, 24, 64, 384, 128
SIDE = [r // 4 for r in range(N)]
GCOL = [r % 4 for r in range(N)]
PAIR = 2 * CJ
BA = CJ + CI
SA = N * CI
KA, KB, KI, KJ = 3, 16, 8, 24
LB, LA, LI, LJ = 0, 16, 20, 28
KO = 20

OPT = dict(order=["aoc+axc", "aos+axs", "foc+fxc", "fos+fxs", "xnc+mtc+snc", "xns+mts+sns"], batches="mnff",
           at={"aoc": 0, "aos": 1, "axc": 5, "axs": 6, "foc": 3, "fos": 4, "fxc": 2, "fxs": 6, "snc": 0, "sns": 1},
           fills=[3, 0], near_v=3, tail_v="c0 c1 g0 g1 d0 d1 e0 e1 t0 t1", tail_s="c0 c1 g0 g1 s0 s1", afirst=True, one=False)

NEAR = 0
MATE = NEAR + 2 * BA
RUN = MATE + CJ
XN = RUN + SA - CI
SN = XN + BA
FARB = SN + CJ
FAR = FARB + 2 * PAIR
BOTH = FAR + PAIR
LW = BOTH + 128

JOBS = [x + k for x in ("ao", "ax", "fo", "fx", "sn", "xn", "mt") for k in "cs"]
SCRATCH = {
    "wa": ("sbuf", [128, 4 * TA], "bfloat16"),
    "wb": ("sbuf", [128, 4 * TB], "bfloat16"),
    "lists": ("sbuf", [128, LJ + KJ], "int32"),
    "off": ("sbuf", [128, 4 * KO], "uint16"),
    "ta": ("sbuf", [128, 4 * 128], "bfloat16"),
    "tf": ("sbuf", [128, 4 * PAIR], "bfloat16"),
    "tn": ("sbuf", [128, 4 * 2 * BA], "bfloat16"),
    "lc": ("sbuf", [128, LW], "float8_e4m3fn_x4"),
    "ls": ("sbuf", [128, LW], "uint8"),
    "quarter": ("sbuf", [128, 1], "float32"),
    "wi": ("sbuf", [128, 10 * KI], "int32"),
    "wj": ("sbuf", [128, 20 * KJ], "int32"),
    "pio": ("sbuf", [128, 4 * KI], "uint16"),
    "pjo": ("sbuf", [128, KJ], "uint16"),
    "prod": ("sbuf", [128, 4 * SA], "float32"),
    "got": ("sbuf", [128, 512], "float32"),
    "put": ("sbuf", [128, 512], "float32"),
    "rows": ("sbuf", [128, 512], "float32"),
    "yy": ("sbuf", [128, JW], "float32"),
    "ps": ("psum", [128, 4 * 512], "float32"),
}
SCRATCH.update({"h" + j: ("sbuf", [128, BA + 8], "float8_e4m3fn_x4" if j[-1] == "c" else "uint8") for j in JOBS})
SEMAPHORES = (["ls", "lp", "lda", "ldb", "zeros", "sp", "ov", "os", "av", "as", "fv", "fs", "nv", "ns", "moved",
               "qa", "qf", "qn", "ii", "jj", "run", "wf", "wm", "wn", "sent", "m0", "m1", "m2", "m3", "tv", "yv", "ys", "stored"]
              + ["G0", "G1", "G2", "G3", "P1", "P2", "P3"] + JOBS + [x + h + e for x in "cgmh" for h in "01" for e in "vs"])


def groups(topo, q):
    chip = [topo.chip(c) for c in CORES]
    mate = [d for d in range(N) if topo.mates(chip[q], chip[d])][0]
    same = [d for d in range(N) if d != q and topo.same_plane(chip[q], chip[d])]
    cross = [d for d in range(N) if d not in same + [q, mate]]
    sn, xn = [d for d in same if GCOL[d] == GCOL[q]][0], [d for d in cross if GCOL[d] == GCOL[mate]][0]
    return mate, sn, [d for d in same if d != sn], xn, [d for d in cross if d != xn]


def places(topo, d):
    mate, sn, sf, xn, xf = groups(topo, d)
    order = [mate] + [q % N for q in range(mate, mate + N) if q % N not in (mate, xn)] + [xn]
    a = {q: RUN + CI * i for i, q in enumerate(order)}
    b = {d: MATE - CJ, mate: MATE, xn: XN + CI, sn: SN}
    b.update({q: FARB + CJ * i for i, q in enumerate(sf + xf)})
    return a, b


def jobs(topo, q):
    mate, sn, sf, xn, xf = groups(topo, q)
    fcol = lambda ds: FAR + CJ * sorted([GCOL[sf[0]], GCOL[xf[0]]]).index(GCOL[ds[0]])
    a = lambda ds: (BOTH, 2 * CI, [(d, CI * SIDE[d], CI, places(topo, d)[0][q], "run") for d in ds])
    f = lambda ds: (fcol(ds), CJ, [(d, 0, CJ, places(topo, d)[1][q], "wf") for d in ds])
    return {"ao": a(sf + [sn]), "ax": a(xf), "fo": f(sf), "fx": f(xf), "sn": (NEAR + BA, BA, [(sn, CI, CJ, SN, "wn")]),
            "xn": (NEAR, BA, [(xn, 0, BA, XN, "wn")]), "mt": (NEAR + CI, BA, [(mate, 0, BA, MATE, "wm")])}


def split(topo, src, ready, parts):
    width = lambda t: t[2] * (4 if t[3][-1] == "c" else 1)
    cs = []
    for w in sorted({width(t) for t in parts}, reverse=True):
        off = [t for t in parts if width(t) == w and topo.chip(t[0]) != topo.chip(src)]
        on = [t for t in parts if width(t) == w and t not in off]
        more = [off[i:i + 2] for i in range(0, len(off), 2)] or [[]]
        more[0] += on
        cs += more
    return [(ready if i == 0 else [], c) for i, c in enumerate(cs)]


def plan(topo, q):
    me, what = CORES[q], jobs(topo, q)
    helpers = sorted([c for c in topo.cores_of(me) if c != me], key=lambda c: topo.die(c) != topo.die(me))
    calls, seen = {me: []}, []
    for entry in OPT["order"]:
        tiles = sorted({"q" + {"a": "a", "f": "f"}.get(j[0], "n") for j in entry.split("+")})
        ready = [x for x in tiles if x not in seen]
        seen += tiles
        tr = []
        for job in entry.split("+"):
            col, w, to = what[job[:2]]
            own = "l" + job[2]
            out = lambda buf, c: [(CORES[d], s, n, buf, c + o, own, at) for d, o, n, at, s in to]
            if job in OPT["at"]:
                h = helpers[OPT["at"][job]]
                tr.append((h, job, w, own, col, "h" + job, 0))
                calls.setdefault(h, []).extend(split(topo, h, [job], out("h" + job, 0)))
            else:
                tr += out(own, col)
        calls[me] += split(topo, me, ready, tr)
    return calls


def masks(topo, src, parts):
    off = [i for i, x in enumerate(parts) if topo.chip(x[0]) != topo.chip(src)]
    on = [i for i in range(len(parts)) if i not in off]
    eoff = topo.engines(src, parts[off[0]][0]) if off else []
    eon = [e for e in topo.engines(src, parts[on[0]][0]) if e not in eoff] if on else []
    share = {i: e[k::len(xs)] for xs, e in ((off, eoff), (on, eon)) for k, i in enumerate(xs)}
    return [sum(1 << e for e in share[i]) for i in range(len(parts))]


def engines_in(m):
    return bin(m).count("1")


def view(T, name, c, w):
    return T[name][:, c:c + w].bitcast(dt.uint8) if name[-1] == "c" else T[name][:, c:c + w]


def arrivals(topo, core):
    n = {}
    for q in range(N):
        for c, calls in plan(topo, q).items():
            for ready, parts in calls:
                for x, m in zip(parts, masks(topo, c, parts)):
                    if x[0] == core:
                        n[x[1]] = n.get(x[1], 0) + engines_in(m)
    return n


def remote_calls(g, core, T, topo, q):
    counts, used = arrivals(topo, core), 0
    for ready, parts in plan(topo, q).get(core, []):
        for s in ready:
            g.wait_ge(T.sem[s], counts.get(s, 1))
        tr = []
        for (c, sem, w, s, sc, d, dc), m in zip(parts, masks(topo, core, parts)):
            rid, pid, _ = topo.addr(c)
            tr.append(RemoteDMATransfer(dst_ids=[DstId(rid=rid, pnc=pid)], dma_engine_mask=m, remote_sem=T.sem[sem],
                                        srcs=[view(T, s, sc, w)], dsts=[view(T, d, dc, w)], alu_op=0))
            used += engines_in(m)
        g.remote_dma_fused(tr, local_sem=T.sem.sent)
    if used:
        g.wait_ge(T.sem.sent, used)


def rank_program(g, core, T, topo):
    rank = T.rank_of(core)
    for q in range(N):
        if topo.chip(CORES[q]) == topo.chip(core):
            remote_calls(g, core, T, topo, q)
    if rank is None:
        return
    v, sc, sy, te, sem = g.vector, g.scalar, g.sync, g.tensor, T.sem
    COPY, A = ActivationFunctionType.Copy, AluOpType
    mate, sn, sf, xn, xf = groups(topo, rank)
    aat, bat = places(topo, rank)
    starts = {"m": [MATE - CJ], "n": [XN + CI], "f": [FARB, FARB + PAIR]}
    wins = [(x, starts[x].pop(0)) for x in OPT["batches"]]
    side = SIDE[rank]
    eng = {"v": v, "s": sc}

    def lists(q, k, c, t, s):
        q.dma_start(T.lists[16 * k:16 * k + 16, c:c + t.shape[1]], t[:]).then_inc(sem[s], 16)
    for c, t in ((LA, T.sa), (LB, T.sb)):
        lists(sy, 0, c, t, "ls")
        lists(sc, 1, c, t, "ls")
    for x in ("ab" if OPT["afirst"] else "ba"):
        sy.dma_start(T["w" + x][:], T[x][:]).then_inc(sem["ld" + x], 16)
    for c, t in ((LI, T.pi), (LJ, T.pj)):
        lists(sc, 0, c, t, "lp")
        lists(sc, 1, c, t, "lp")
    sy.wait_ge(sem.qa, 1)
    for name in ("lc", "ls"):
        sy.dma_start(view(T, name, aat[rank], CI), view(T, name, BOTH + CI * side, CI)).then_inc(sem.moved, 16)

    n = {}

    def inc(ins, s):
        ins.then_inc(sem[s], 1)
        n[s] = n.get(s, 0) + 1

    def wait(e, *ss):
        for s in ss:
            e.wait_ge(sem[s], n[s])

    def move(who, o, i, s):
        inc(v.tensor_copy(o, i) if who == "v" else sc.activation(o, i, COPY), s + who)

    wi = lambda j, w=1, p=0: T.wi[p:p + 32, KI * j:KI * (j + w)]
    wj = lambda j, w=1: T.wj[:, KJ * j:KJ * (j + w)]
    pi, pj = T.lists[0:32, LI:LI + KI], T.lists[:, LJ:LJ + KJ]
    d = [aat[r] - RUN - CI * r for r in range(N)]
    jumps = ([r for r in range(1, N) if d[r] != d[r - 1]] + [0, 0, 0])[:3]
    k_of = {r: [i for i, (x, c) in enumerate(wins) if c <= bat[r] < c + PAIR][0] for r in range(N)}
    e = [512 - 4 * (bat[r] - wins[k_of[r]][1]) + 32 * k_of[r] - CJ * r for r in range(N)]
    ts, tt, tc = v.tensor_scalar, v.tensor_tensor, v.tensor_copy
    nk = 4 if OPT["one"] else 2
    chain_i = [[(ts, wi(0), pi, d[0], None, A.add)]
               + [(ts, wi(1 + j), pi, CI * r, d[r] - d[r - 1] if r else 0, A.is_ge, A.mult) for j, r in enumerate(jumps)],
               [(tt, wi(4, 2), wi(0, 2), wi(2, 2), A.add)],
               [(tt, wi(6), wi(4), wi(5), A.add), (tt, wi(7), wi(4), wi(5), A.add)],
               [(tc, wi(8, 1, 32 * a), T.wi[0:32, 6 * KI + 2 * a:7 * KI + 2 * a]) for a in range(4)],
               [(ts, T.pio[:, 2 * k + h:KI * nk:2 * nk], T.wi[:, 8 * KI + h:9 * KI:2], SA * k, None, A.add) for k in range(nk) for h in range(2)]]
    chain_j = [[(tc, T.lists[p:p + 32, LJ:LJ + KJ], T.lists[0:32, LJ:LJ + KJ]) for p in (32, 64, 96)],
               [(ts, wj(16), pj, 32, None, A.bitwise_and), (ts, wj(0), pj, T.quarter[:, 0:1], None, A.add)]
               + [(ts, wj(r), pj, CJ * r, e[r] - e[r - 1], A.is_ge, A.mult) for r in range(1, N)],
               [(ts, wj(17), wj(16), -5, None, A.mult), (tt, wj(8, 4), wj(0, 4), wj(4, 4), A.add)],
               [(tt, wj(12, 2), wj(8, 2), wj(10, 2), A.add)], [(tt, wj(14), wj(12), wj(13), A.add)],
               [(tt, wj(15), wj(14), wj(17), A.add)], [(ts, wj(18), wj(15), 511, None, A.bitwise_and)], [(tc, T.pjo[:], wj(18))]]
    todo = []
    for tok in "j0 i0 j1 i1 j2 i2 j3 i3 j4 i4 j5 j6 j7".split():
        todo += [(2 * tok[0], i == 0, op) for i, op in enumerate((chain_i if tok[0] == "i" else chain_j)[int(tok[1])])]

    def fill(k):
        for s, new, op in todo[:k]:
            if s not in n:
                v.wait_ge(sem.lp, 64)
            elif new:
                wait(v, s)
            inc(op[0](*op[1:]), s)
        del todo[:k]

    pieces = {"a": (T.ta, 0, T.wa, LA, KA, "a"), "f": (T.tf, 0, T.wb, 4 * min(GCOL[sf[0]], GCOL[xf[0]]), 8, "f"),
              "m": (T.tn, CI, T.wb, 4 * GCOL[mate], 4, "n"), "o": (T.tn, BA + CI, T.wb, 4 * GCOL[rank], 4, "n")}

    def gather(x, who, ts):
        tl, c, win, k, w, s = pieces[x]
        for t in ts:
            move(who, tl[:, 4 * c + t:4 * (c + 16 * w):4], win[:].indirect(T.off[:, KO * t + k:KO * t + k + w]), s)

    def quantise(x, tl, at, w):
        wait(v, x + "v", x + "s")
        inc(v.quantize_mx(T.lc[:, at:at + w], T.ls[:, at:at + w], tl[:]), "q" + x)

    def both(x):
        for who in "sv":
            wait(eng[who], "ov", "os")
            eng[who].wait_ge(sem["ld" + x.replace("f", "b")], 16)
            gather(x, who, (2, 3) if who == "s" else (0, 1))

    def beside():
        wait(sc, "av", "as")
        for c, s in ((0, 1 - side), (BA, side)):
            move("s", T.tn[:, 4 * c:4 * (c + CI)], T.ta[:, 4 * CI * s:4 * CI * (s + 1)], "n")
    inc(v.memset(T.ta[:, 8 * CI:], 0.0), "zeros")
    for b in range(4):
        inc(v.memset(T.quarter[32 * b:32 * b + 32, :], float(128 * b + e[0])), "zeros")
    wait(v, "zeros")
    v.wait_ge(sem.ls, 64)
    for p in (32, 64, 96):
        inc(v.tensor_copy(T.lists[p:p + 32, 0:KB + KA], T.lists[0:32, 0:KB + KA]), "sp")
    wait(v, "sp")
    for t in (2, 0, 3, 1):
        inc(v.tensor_scalar(T.off[:, KO * t:KO * t + KB + KA], T.lists[:, 0:KB + KA], 4, t, A.mult, A.add), "o" + "vs"[t // 2])
    nv = OPT["near_v"]
    if OPT["afirst"]:
        both("a")
        beside()
        quantise("a", T.ta, BOTH, 128)
        both("f")
        gather("m", "s", range(4))
        gather("o", "s", range(nv, 4))
        fill(OPT["fills"][0])
        quantise("f", T.tf, FAR, PAIR)
        gather("o", "v", range(nv))
    else:
        both("f")
        gather("m", "s", range(2))
        quantise("f", T.tf, FAR, PAIR)
        gather("o", "v", range(1))
        both("a")
        gather("m", "s", range(2, 4))
        beside()
        gather("o", "v", range(1, 2))
        quantise("a", T.ta, BOTH, 128)
        gather("o", "v", range(2, 4))
    fill(OPT["fills"][1])
    quantise("n", T.tn, NEAR, 2 * BA)
    fill(len(todo))

    counts = arrivals(topo, core)
    for s in ("qa", "qf", "qn"):
        te.wait_ge(sem[s], 1)
    te.wait_ge(sem.moved, 32)
    for s in ("run", "wm", "wn"):
        te.wait_ge(sem[s], counts[s])
    for k, (x, c) in enumerate(wins):
        te.wait_ge(sem["w" + x], counts["w" + x])
        te.matmul_mx(T.ps[:, 512 * k:512 * k + SA], T.lc[:, c:c + PAIR], T.ls[:, c:c + PAIR],
                     T.lc[:, RUN:RUN + SA], T.ls[:, RUN:RUN + SA], True, True).then_inc(sem["m%d" % k], 1)

    def blk(buf, h, r, p=0, w=128):
        return buf[p:p + w, 256 * h + 64 * r:256 * h + 64 * r + 64]

    def stage(who, what, h):
        en, H = eng[who], str(h)
        if what == "c":
            k = 2 * h + (who == "s")
            en.wait_ge(sem["m%d" % k], 1)
            move(who, T.prod[:, SA * k:SA * k + SA], T.ps[:, 512 * k:512 * k + SA], "c" + H)
        if what == "g":
            r0, r1 = (0, 3) if who == "s" else (3, 4)
            wait(en, "ii")
            en.wait_ge(sem["c" + H + "v"], 1)
            en.wait_ge(sem["c" + H + "s"], 1)
            move(who, T.got[:, 256 * h + 64 * r0:256 * h + 64 * r1],
                 T.prod[:, 2 * SA * h:2 * SA * (h + 1)].indirect(T.pio[:, 4 * r0:4 * r1]), "g" + H)

        def turn(buf, r, shift, w):
            for p in range(0, 128, w):
                to = (p + shift) % 128
                inc(v.transpose(T.rows[to:to + w, 128 * r + 64 * h:128 * r + 64 * h + 64], blk(buf, h, r, p, w)), "tv")
        if what == "s":
            en.wait_ge(sem["g" + H + "s"], 1)
            for p in range(0, 128, 32):
                move(who, blk(T.put, h, 1, (p + 32) % 128, 32), blk(T.got, h, 1, p, 32), "m" + H)
        if what == "d":
            v.wait_ge(sem["g" + H + "v"], 1)
            turn(T.got, 3, 96, 32)
        if what == "e":
            v.wait_ge(sem["g" + H + "s"], 1)
            turn(T.got, 0, 0, 128)
            turn(T.got, 2, 64, 64)
        if what == "t":
            v.wait_ge(sem["m" + H + "s"], 4)
            turn(T.put, 1, 0, 128)
    def whole(who, what, r):
        en, R = eng[who], str(r)
        quad = lambda buf, p=0, w=128: buf[p:p + w, 128 * r:128 * r + 128]
        copy = v.tensor_copy if who == "v" else lambda o, i: sc.activation(o, i, COPY)
        w = 64 if r == 2 else 32
        if what == "c":
            en.wait_ge(sem["m" + R], 1)
            inc(copy(T.prod[:, SA * r:SA * r + SA], T.ps[:, 512 * r:512 * r + SA]), "c0v")
        if what == "g":
            wait(en, "ii")
            en.wait_ge(sem.c0v, 4)
            inc(copy(quad(T.got), T.prod[:].indirect(T.pio[:, 8 * r:8 * r + 8])), "G" + R)
        if what == "s":
            en.wait_ge(sem["G" + R], 1)
            for p in range(0, 128, w):
                inc(copy(quad(T.put, (p + 32 * r) % 128, w), quad(T.got, p, w)), "P" + R)
        if what == "d":
            en.wait_ge(sem["G" + R], 1)
            for p in range(0, 128, w):
                inc(v.transpose(quad(T.rows, (p + 32 * r) % 128, w), quad(T.got, p, w)), "tv")
        if what == "t":
            v.wait_ge(sem["P" + R if r else "G0"], (1, 4, 2, 4)[r])
            inc(v.transpose(quad(T.rows), quad(T.put if r else T.got)), "tv")
    for who in "vs":
        for tok in OPT["tail_" + who].split():
            (whole if OPT["one"] else stage)(who, tok[0], int(tok[1]))
    hy = JW // 2
    for who, c in (("v", 0), ("s", hy)):
        wait(eng[who], "jj", "tv")
        move(who, T.yy[:, c:c + hy], T.rows[:].indirect(T.pjo[:, c // 16:(c + hy) // 16]), "y")
    wait(sy, "yv", "ys")
    sy.dma_start(T.y[:], T.yy[:]).then_inc(sem.stored, 16)
    sy.wait_ge(sem.stored, 16)
